import numpy as np
CORES = [26,28,98,100,106,108,122,124]
N = 8
T, EL, CAP, CAPP = 1024, 2, 480, 128
E = N * EL
def entries(a): return a.T.reshape(-1)
def pack(v, P): return np.ascontiguousarray(np.asarray(v, np.int32).reshape(-1, P).T)
def lists(rng, how):
    if how == "uniform": return {"ex": np.stack([pack(rng.permutation(np.repeat(np.arange(E), CAPP))[:T], 16) for r in range(N)])}
    R = np.arange(N)[:, None]; c = rng.permutation(E); C = np.zeros((N, E), np.int64)
    if how == "bands":
        a = c % N; C = CAPP * ((R >= a) & (R <= a + CAP // CAPP)); C[a, np.arange(E)] = np.where(c < N, CAPP, rng.integers(1, CAPP + 1, E))
    if how == "full":
        g = T // CAPP; C[:, c[:g]] = CAPP; C[:, c[:g // 2]] = rng.integers(CAPP // 2, CAPP + 1, (N, g // 2))
    if how in ("skew", "sorted"):
        V = np.full((N, 3), CAP // N); V[:, 0] = rng.integers(2, CAP // N + 1, N); h = rng.integers(1, N - 2); V[h, 0] = 0; V[h + 1, 0] = 1; V[rng.integers(N), 1:] += CAP % N; V[rng.integers(N), 2] += 1
        W = rng.random((N, E)) ** 4 + 1e-9; W[:, c[:3]] = 0
        C = np.minimum(((T - T // 8 - V.sum(axis=1, keepdims=True)) * W / W.sum(axis=1, keepdims=True)).astype(np.int64), CAPP); C[:, c[:3]] = V
    if how == "thin":
        C = rng.integers(0, CAP // N + 1, (N, E)); C[1] = 1; C[[0, N // 2, N - 1]] = 0
    X = np.stack([rng.permutation(np.concatenate([np.repeat(np.arange(E), C[r]), np.full(T - C[r].sum(), -1)])) for r in range(N)])
    if how == "sorted": X = np.sort(X, axis=1); X[1::2] = X[1::2, ::-1].copy()
    return {"ex": np.stack([pack(v, 16) for v in X])}
def blank(d):
    for r in range(0, N, 2):
        u, i = np.unique(entries(d["ex"][r])[::-1], return_index=True); d["x"][r][:, T - 1 - i[u >= 0]] = 0
def setup_inputs(rng):
    return dict({"x": rng.standard_normal((N, 128, T), dtype=np.float32)}, **lists(rng, "uniform"))
def setup_inputs_bands(rng):
    d = setup_inputs(rng); d.update(lists(rng, "bands"))
    for k in ("x",): d[k] = (d[k].astype(np.float32) * 1048576.0).astype(d[k].dtype)
    blank(d)
    return d
def setup_inputs_full(rng):
    d = setup_inputs(rng); d.update(lists(rng, "full"))
    for k in ("x",): d[k] = (d[k].astype(np.float32) * (1 / 1024.0)).astype(d[k].dtype)
    blank(d)
    return d
def setup_inputs_skew(rng):
    d = setup_inputs(rng); d.update(lists(rng, "skew"))
    blank(d)
    return d
def setup_inputs_sorted(rng):
    d = setup_inputs(rng); d.update(lists(rng, "sorted"))
    blank(d)
    return d
def setup_inputs_thin(rng):
    d = setup_inputs(rng); d.update(lists(rng, "thin"))
    blank(d)
    return d
def check_inputs(x):
    bad = []
    if x["ex"].min() < -1 or x["ex"].max() >= E: bad.append("ex out of range")
    if max(int(np.bincount(entries(a)[entries(a) >= 0], minlength=E).max()) for a in x["ex"]) > CAPP: bad.append("more than CAPP tokens of one rank choose one expert")
    return bad
def reference(x, ex):
    X = np.concatenate(list(x), axis=1); e = np.concatenate([entries(a) for a in ex])
    k = np.nonzero(e >= 0)[0]; o = k[np.argsort(e[k], kind="stable")]; s = e[o]
    p = np.arange(len(o)) - np.searchsorted(s, s)
    Y = np.zeros((128, E * CAP), x.dtype); m = p < CAP; Y[:, CAP * s[m] + p[m]] = X[:, o[m]]
    return {"y": np.stack([Y[:, EL * CAP * r:EL * CAP * (r + 1)] for r in range(N)])}

@@ -1,0 +1,372 @@
+from concourse.bass import DstId, RemoteDMATransfer
+from concourse.mybir import AluOpType, AxisListType, ActivationFunctionType
+
+SIM = 128
+N, EL, CAP, CAPP = 8, 2, 480, 128
+BLK = EL * CAPP
+ZC = CAPP + CAP
+LW = N * BLK + ZC
+HALF = 256
+
+SCRATCH = {
+    "exall": ("dram", [N, 128, 8], "int32"),
+    "xs": ("sbuf", [128, 1024], "float32"),
+    "sb": ("sbuf", [128, N * BLK], "float32"),
+    "land": ("sbuf", [128, LW], "float32"),
+    "rb": ("sbuf", [128, 2 * BLK], "float32"),
+    "y0": ("sbuf", [128, CAP], "float32"),
+    "y1": ("sbuf", [128, CAP], "float32"),
+    "ext": ("sbuf", [128, 8], "int32"),
+    "xa": ("sbuf", [128, 64], "int32"),
+    "pcol": ("sbuf", [128, 1], "int32"),
+    "ti": ("sbuf", [128, 8], "int32"),
+    "tu": ("sbuf", [128, 8], "uint16"),
+    "mu": ("sbuf", [128, 8], "uint16"),
+    "pi": ("sbuf", [128, 4], "int32"),
+    "pf": ("sbuf", [128, 4], "float32"),
+    "sc": ("sbuf", [128, 4], "float32"),
+    "wf": ("sbuf", [128, 128], "bfloat16"),
+    "kf": ("sbuf", [128, 128], "bfloat16"),
+    "n16": ("sbuf", [128, 128], "bfloat16"),
+    "rf": ("sbuf", [128, 128], "bfloat16"),
+    "c16": ("sbuf", [128, 60], "float32"),
+    "ma": ("sbuf", [128, 128], "bfloat16"),
+    "mab": ("sbuf", [128, 128], "bfloat16"),
+    "mac": ("sbuf", [128, 128], "bfloat16"),
+    "mb": ("sbuf", [128, 128], "bfloat16"),
+    "mc": ("sbuf", [128, 128], "bfloat16"),
+    "rst": ("sbuf", [128, 128], "float32"),
+    "brow": ("sbuf", [128, 128], "bfloat16"),
+    "ones": ("sbuf", [128, 128], "bfloat16"),
+    "jc": ("sbuf", [128, 8], "float32"),
+    "oh": ("sbuf", [128, 128], "bfloat16"),
+    "t1": ("sbuf", [128, 64], "bfloat16"),
+    "t2": ("sbuf", [128, 32], "bfloat16"),
+    "t3": ("sbuf", [128, 16], "bfloat16"),
+    "trep": ("sbuf", [128, 128], "bfloat16"),
+    "q": ("sbuf", [128, 128], "float32"),
+    "vs": ("sbuf", [128, 128], "float32"),
+    "ni": ("sbuf", [128, 8], "int32"),
+    "v16": ("sbuf", [128, 8], "float32"),
+    "lh": ("sbuf", [128, 1024], "float16"),
+    "rh": ("sbuf", [128, 1024], "float16"),
+    "offs": ("sbuf", [128, 128], "uint16"),
+    "le": ("sbuf", [128, 128], "bfloat16"),
+    "eq": ("sbuf", [128, 128], "bfloat16"),
+    "rr": ("sbuf", [128, 128], "float16"),
+    "bas": ("sbuf", [128, 60], "float16"),
+    "ip": ("sbuf", [128, 30], "float32"),
+    "eqx": ("sbuf", [128, 128], "float32"),
+    "cnf": ("sbuf", [128, 2], "float32"),
+    "cnb": ("sbuf", [128, 2], "bfloat16"),
+    "dl": ("sbuf", [128, 2], "float32"),
+    "st": ("sbuf", [128, 60], "float16"),
+    "ro": ("sbuf", [128, 60], "uint16"),
+    "pcum": ("psum", [128, 512], "float32"),
+    "pidx": ("psum", [128, 512], "float32"),
+    "pcnt": ("psum", [128, 512], "float32"),
+    "prix": ("psum", [128, 512], "float32"),
+}
+SEMAPHORES = (["meta", "data", "loc", "exs", "exd", "xl", "xal", "sta", "stb"]
+              + ["gi%d" % i for i in range(7)] + ["p1", "p2", "p3", "p4", "k1", "k3", "kz"]
+              + ["o1", "u1", "u2", "u3", "u4", "m1", "m2", "m3", "m4", "q1", "q2", "q3", "q4", "of"]
+              + ["b%d" % i for i in range(8)] + ["gv%d" % i for i in range(4)] + ["gs%d" % i for i in range(4)]
+              + ["r1", "r2", "r3", "r4", "r5", "r6", "yva", "yvb", "ysa", "ysb"])
+
+
+def bits(m):
+    return [i for i in range(m.bit_length()) if m >> i & 1]
+
+
+def join(b):
+    return sum(1 << i for i in b)
+
+
+def routes(cores, topo):
+    chips = []
+    for c in cores:
+        if topo.chip(c) not in chips:
+            chips.append(topo.chip(c))
+    allchips = sorted({topo.chip(c) for c in range(SIM)})
+    mate = {a: b for a in allchips for b in allchips if topo.mates(a, b)}
+    on = {x: [i for i, c in enumerate(cores) if topo.chip(c) == x] for x in chips}
+    used = set(cores)
+
+    def relay(chip, die, dst):
+        h = [c for c in range(SIM) if topo.chip(c) == chip and topo.die(c) == die and c not in used
+             and topo.may_write(c, dst)][0]
+        used.add(h)
+        return h
+
+    plan = []
+    for src in cores:
+        cs = topo.chip(src)
+        todo = []
+        for x in chips:
+            if x == cs:
+                continue
+            dst = cores[on[x][0]]
+            rot = (chips.index(x) - chips.index(cs)) % len(chips)
+            h = None
+            if not topo.same_plane(cs, x):
+                if not topo.mates(cs, x) and mate[cs] in chips:
+                    h = relay(mate[x], topo.die(src), dst)
+                elif not topo.may_write(src, dst):
+                    h = relay(cs, topo.die(src), dst)
+            kind = 2 if h is None else (1 if topo.chip(h) == cs else 0)
+            todo.append((kind, rot, on[x], h))
+        todo.sort(key=lambda a: a[:2])
+        plan.append([(a[2], a[3]) for a in todo])
+    return plan
+
+
+def masks(core, topo):
+    away = [c for c in range(SIM) if topo.chip(c) != topo.chip(core) and topo.may_write(core, c)][0]
+    near = [c for c in range(SIM) if topo.chip(c) == topo.chip(core) and c != core][0]
+    off = bits(topo.mask(core, away))
+    return off, [i for i in bits(topo.mask(core, near)) if i not in off]
+
+
+def ident(topo, c):
+    rid, pid, _ = topo.addr(c)
+    return DstId(rid=rid, pnc=pid)
+
+
+def pair(topo, src_aps, dst_aps, dsts, eng, sem):
+    h = len(eng) // 2
+    return [RemoteDMATransfer(dst_ids=[ident(topo, dsts[i])], dma_engine_mask=join(eng[i * h:(i + 1) * h]),
+                              remote_sem=sem, srcs=[src_aps[i]], dsts=[dst_aps[i]]) for i in range(2)]
+
+
+def cast(T, topo, r, dsts, eng):
+    return RemoteDMATransfer(dst_ids=[ident(topo, d) for d in dsts], dma_engine_mask=join(eng), remote_sem=T.sem.meta,
+                             srcs=[T.exall[r]], dsts=[T.exall[r] for d in dsts])
+
+
+def relay_program(g, core, T, topo, r, ranks):
+    cores = T.cores
+    off, near = masks(core, topo)
+    came = near if topo.chip(cores[r]) == topo.chip(core) else masks(cores[r], topo)[0]
+    dsts = [cores[d] for d in ranks]
+    g.wait_ge(T.sem.meta, len(came))
+    g.remote_dma_fused([cast(T, topo, r, dsts, off)], local_sem=T.sem.loc)
+    g.wait_ge(T.sem.data, len(came))
+    g.remote_dma_fused(pair(topo, [T.rb[:, i * BLK:(i + 1) * BLK] for i in range(2)],
+                            [T.land[:, r * BLK:(r + 1) * BLK]] * 2, dsts, off, T.sem.data), local_sem=T.sem.loc)
+    g.wait_ge(T.sem.loc, 2 * len(off))
+
+
+def rank_program(g, core, T, topo):
+    cores = list(T.cores)
+    plan = routes(cores, topo)
+    rank = T.rank_of(core)
+    if rank is None:
+        for r in range(N):
+            for ranks, h in plan[r]:
+                if h == core:
+                    relay_program(g, core, T, topo, r, ranks)
+        return
+    S = T.sem
+    V, A, P, Y = g.vector, g.scalar, g.tensor, g.sync
+    op = AluOpType
+    mine = plan[rank]
+    partner = [i for i, c in enumerate(cores) if topo.chip(c) == topo.chip(core) and i != rank][0]
+    off, near = masks(core, topo)
+    meta_total = len(near)
+    data_total = len(near)
+    for r in range(N):
+        for ranks, h in plan[r]:
+            if rank in ranks:
+                eng = masks(h if h is not None else cores[r], topo)[0]
+                meta_total += len(eng)
+                data_total += len(eng) // 2
+
+    Y.dma_start(T.ext[:, :], T.ex[:, :]).then_inc(S.exs, 16)
+    A.dma_start(T.exall[rank], T.ex[:, :]).then_inc(S.exd, 16)
+    Y.dma_start(T.xs[:, :], T.x[:, :]).then_inc(S.xl, 16)
+
+    imp = {"allow_small_or_imprecise_dtypes": True}
+    g.iota(T.pcol[:, :], [[0, 1]], 0, 1).then_inc(S.gi0, 1)
+    g.iota(T.wf[:, :], [[1, 16], [16, 8]], 0, 0, **imp).then_inc(S.gi1, 1)
+    g.iota(T.ti[:, :], [[1, 8]], 0, 0).then_inc(S.gi2, 1)
+    g.iota(T.kf[:, :], [[0, 8], [1, 16]], 0, 0, **imp).then_inc(S.gi3, 1)
+    g.iota(T.n16[:, :], [[16, 128]], 16, 0, **imp).then_inc(S.gi4, 1)
+    g.iota(T.rf[:, :], [[1, 8], [0, 16]], 0, 0, **imp).then_inc(S.gi5, 1)
+    g.iota(T.c16[:, :], [[128, 2], [16, 30]], 0, 0, **imp).then_inc(S.gi6, 1)
+    out_, in_ = [], [cores[partner]]
+    for ranks, h in mine:
+        if h is None:
+            out_ += [cores[d] for d in ranks]
+        elif topo.chip(h) == topo.chip(core):
+            in_.append(h)
+        else:
+            out_.append(h)
+    g.wait_ge(S.exd, 16)
+    g.remote_dma_fused([cast(T, topo, rank, out_, off), cast(T, topo, rank, in_, near)], local_sem=S.loc)
+    loc = len(off) + len(near)
+    for i, (ranks, h) in enumerate(mine):
+        g.wait_ge(S["gv%d" % i], 1)
+        g.wait_ge(S["gs%d" % i], 1)
+        a = ranks[0] * BLK
+        if h is None:
+            g.remote_dma_fused(pair(topo, [T.sb[:, d * BLK:(d + 1) * BLK] for d in ranks],
+                                    [T.land[:, rank * BLK:(rank + 1) * BLK]] * 2, [cores[d] for d in ranks], off, S.data),
+                               local_sem=S.loc)
+            loc += len(off)
+        else:
+            eng = near if topo.chip(h) == topo.chip(core) else off
+            rid, pid, _ = topo.addr(h)
+            g.remote_dma(T.rb[:, :], T.sb[:, a:a + 2 * BLK], S.data, S.loc, pid, rid, join(eng))
+            loc += len(eng)
+    g.wait_ge(S.gv3, 1)
+    rid, pid, _ = topo.addr(cores[partner])
+    g.remote_dma(T.land[:, rank * BLK:(rank + 1) * BLK], T.sb[:, partner * BLK:(partner + 1) * BLK], S.data, S.loc,
+                 pid, rid, join(near))
+    loc += len(near)
+
+    V.wait_ge(S.gi0, 1)
+    for i, (o, n) in enumerate([(op.bitwise_and, 7), (op.logical_shift_right, 3), (op.bitwise_and, 15),
+                                (op.logical_shift_right, 4)]):
+        V.tensor_scalar(T.pi[:, i:i + 1], T.pcol[:, :], n, None, o).then_inc(S.p1, 1)
+    V.wait_ge(S.p1, 4)
+    V.tensor_copy(T.pf[:, :], T.pi[:, :]).then_inc(S.p2, 1)
+    V.wait_ge(S.p2, 1)
+    V.tensor_scalar(T.sc[:, 0:1], T.pf[:, 0:1], 16.0, None, op.mult).then_inc(S.p3, 1)
+    V.tensor_scalar(T.sc[:, 1:2], T.pf[:, 0:1], 16.0, 15.0, op.mult, op.add).then_inc(S.p3, 1)
+    V.tensor_scalar(T.sc[:, 2:3], T.pf[:, 0:1], 16.0, T.pf[:, 1:2], op.mult, op.add).then_inc(S.p3, 1)
+    V.tensor_scalar(T.sc[:, 3:4], T.pf[:, 0:1], 128.0, T.pf[:, 1:2], op.mult, op.add).then_inc(S.p3, 1)
+    V.wait_ge(S.p3, 4)
+    V.wait_ge(S.gi1, 1)
+    V.tensor_scalar(T.ma[:, :], T.wf[:, :], T.sc[:, 1:2], None, op.is_gt).then_inc(S.p4, 1)
+    V.tensor_scalar(T.mab[:, :], T.wf[:, :], T.sc[:, 0:1], None, op.is_ge).then_inc(S.p4, 1)
+    V.tensor_scalar(T.mac[:, :], T.wf[:, :], T.sc[:, 2:3], None, op.is_gt).then_inc(S.p4, 1)
+    V.wait_ge(S.gi2, 1)
+    V.tensor_copy(T.tu[:, :], T.ti[:, :]).then_inc(S.k1, 1)
+    V.tensor_scalar(T.mu[:, :], T.ti[:, :], 0.0, T.pf[:, 2:3], op.mult, op.add).then_inc(S.k1, 1)
+    V.tensor_scalar(T.jc[:, :], T.ti[:, :], 16.0, T.sc[:, 3:4], op.mult, op.add).then_inc(S.k1, 1)
+    V.wait_ge(S.p4, 3)
+    V.tensor_tensor(T.mb[:, :], T.mab[:, :], T.ma[:, :], op.subtract).then_inc(S.k1, 1)
+    V.tensor_tensor(T.mc[:, :], T.mac[:, :], T.ma[:, :], op.subtract).then_inc(S.k1, 1)
+    V.memset(T.ones[:, :], 1.0).then_inc(S.k1, 1)
+    V.wait_ge(S.gi3, 1)
+    V.tensor_scalar(T.rst[:, :], T.kf[:, :], 0.0, None, op.is_gt).then_inc(S.k1, 1)
+    V.tensor_scalar(T.brow[:, :], T.kf[:, :], 128.0, 16.0, op.mult, op.add).then_inc(S.k1, 1)
+    K1 = 8
+    V.wait_ge(S.k1, K1)
+    V.wait_ge(S.exs, 16)
+    V.tensor_tensor(T.oh[:, :], T.ext[:, 0:8].indirect(T.tu[:, 0:8]), T.kf[:, :], op.is_equal).then_inc(S.o1, 1)
+    V.wait_ge(S.o1, 1)
+    V.tensor_tensor(T.t1[:, :], T.oh[:, 0:64], T.oh[:, 64:128], op.add).then_inc(S.u1, 1)
+    V.wait_ge(S.u1, 1)
+    V.tensor_tensor(T.t2[:, :], T.t1[:, 0:32], T.t1[:, 32:64], op.add).then_inc(S.u2, 1)
+    V.wait_ge(S.u2, 1)
+    V.tensor_tensor(T.t3[:, :], T.t2[:, 0:16], T.t2[:, 16:32], op.add).then_inc(S.u3, 1)
+    V.wait_ge(S.u3, 1)
+    V.tensor_copy(T.trep[:, :], T.t3[:, 0:16].indirect(T.mu[:, 0:8])).then_inc(S.u4, 1)
+    V.wait_ge(S.m1, 1)
+    V.tensor_tensor(T.q[:, :], T.oh[:, :], T.pcum[:, 0:128], op.mult).then_inc(S.q1, 1)
+    V.wait_ge(S.q1, 1)
+    V.tensor_tensor_scan(T.vs[:, :], T.rst[:, :], T.q[:, :], 0.0, op.mult, op.add).then_inc(S.q2, 1)
+    V.wait_ge(S.q2, 1)
+    V.tensor_scalar(T.ni[:, :], T.vs[:, 15::16], 0.0625, -0.46875, op.mult, op.add).then_inc(S.q3, 1)
+    V.wait_ge(S.q3, 1)
+    V.tensor_scalar(T.v16[:, :], T.ni[:, :], 16.0, None, op.mult).then_inc(S.q4, 1)
+    V.wait_ge(S.gi4, 1)
+    V.wait_ge(S.q4, 1)
+    for t in range(8):
+        c = slice(128 * t, 128 * (t + 1))
+        V.tensor_scalar(T.lh[:, c], T.kf[:, :], T.v16[:, t:t + 1], T.vs[:, 16 * t + 15:16 * t + 16], op.add,
+                        op.is_equal).then_inc(S["b%d" % t], 1)
+        V.tensor_scalar(T.rh[:, c], T.n16[:, :], T.v16[:, t:t + 1], T.jc[:, t:t + 1], op.is_equal,
+                        op.mult).then_inc(S["b%d" % t], 1)
+    V.wait_ge(S.m2, 1)
+    V.tensor_copy(T.offs[:, :], T.pidx[:, 0:128]).then_inc(S.of, 1)
+
+    P.wait_ge(S.p4, 3)
+    P.wait_ge(S.k1, K1)
+    P.matmul(T.pcum[:, 0:128], T.ones[0:1, :], T.brow[0:1, :], True, False)
+    P.wait_ge(S.o1, 1)
+    P.matmul(T.pcum[:, 0:128], T.mc[:, :], T.oh[:, :], False, False)
+    for d in range(1, 8):
+        P.matmul(T.pcum[:, 16 * d:128], T.mb[:, :], T.oh[:, 0:128 - 16 * d], False, False)
+    P.wait_ge(S.u4, 1)
+    P.matmul(T.pcum[:, 0:128], T.ma[:, :], T.trep[:, :], False, True).then_inc(S.m1, 1)
+    for t in range(8):
+        c = slice(128 * t, 128 * (t + 1))
+        P.wait_ge(S["b%d" % t], 2)
+        m = P.matmul(T.pidx[:, 0:128], T.lh[:, c], T.rh[:, c], t == 0, t == 7)
+    m.then_inc(S.m2, 1)
+
+    def pack(eng, d, out, sem):
+        src = T.xs[:, 0:1024].indirect(T.offs[:, 16 * d:16 * (d + 1)])
+        if eng == "v":
+            V.tensor_copy(out, src).then_inc(sem, 1)
+        else:
+            A.activation(out, src, ActivationFunctionType.Copy).then_inc(sem, 1)
+
+    for e in (V, A):
+        e.wait_ge(S.of, 1)
+        e.wait_ge(S.xl, 16)
+    for i, (ranks, h) in enumerate(mine):
+        u, v = ranks
+        pack("v", u, T.sb[:, u * BLK:(u + 1) * BLK], S["gv%d" % i])
+        pack("s", v, T.sb[:, v * BLK:(v + 1) * BLK], S["gs%d" % i])
+    pack("v", partner, T.sb[:, partner * BLK:(partner + 1) * BLK], S.gv3)
+    pack("s", rank, T.land[:, rank * BLK:(rank + 1) * BLK], S.gs3)
+
+    Y.wait_ge(S.exd, 16)
+    Y.wait_ge(S.meta, meta_total)
+    Y.dma_start(T.xa[:, :], T.exall[:, :, :]).then_inc(S.xal, 16)
+    V.memset(T.land[:, N * BLK:LW], 0.0).then_inc(S.kz, 1)
+    V.wait_ge(S.gi5, 1)
+    V.wait_ge(S.gi6, 1)
+    V.tensor_scalar(T.le[:, :], T.rf[:, :], T.pf[:, 3:4], None, op.is_ge).then_inc(S.k3, 1)
+    V.tensor_scalar(T.eq[:, :], T.rf[:, :], T.pf[:, 3:4], None, op.is_equal).then_inc(S.k3, 1)
+    V.tensor_scalar(T.rr[:, :], T.kf[:, :], T.pf[:, 2:3], None, op.is_equal).then_inc(S.k3, 1)
+    V.tensor_scalar(T.bas[:, :], T.c16[:, :], T.pf[:, 2:3], None, op.add).then_inc(S.k3, 1)
+    V.tensor_scalar(T.ip[:, :], T.c16[:, 0:30], T.pf[:, 2:3], None, op.add).then_inc(S.k3, 1)
+    V.wait_ge(S.xal, 16)
+    for e in range(EL):
+        V.tensor_scalar(T.eqx[:, 64 * e:64 * (e + 1)], T.xa[:, :], float(EL * rank + e), None,
+                        op.is_equal).then_inc(S.r1, 1)
+    V.wait_ge(S.r1, 2)
+    for e in range(EL):
+        V.tensor_reduce(T.cnf[:, e:e + 1], T.eqx[:, 64 * e:64 * (e + 1)], AxisListType.X, op.add).then_inc(S.r2, 1)
+    V.wait_ge(S.r2, 2)
+    V.tensor_copy(T.cnb[:, :], T.cnf[:, :]).then_inc(S.r3, 1)
+    P.wait_ge(S.k3, 5)
+    P.matmul(T.prix[:, 0:60], T.rr[0:16, :], T.bas[0:16, :], True, False)
+    P.wait_ge(S.r3, 1)
+    P.matmul(T.pcnt[:, 0:2], T.le[:, :], T.cnb[:, :], True, True)
+    P.matmul(T.pcnt[:, 2:4], T.eq[:, :], T.cnb[:, :], True, True).then_inc(S.m3, 1)
+    V.wait_ge(S.k3, 5)
+    V.wait_ge(S.m3, 1)
+    V.tensor_scalar(T.dl[:, :], T.pcnt[:, 2:4], -1.0, float(BLK), op.mult, op.add).then_inc(S.r4, 1)
+    V.wait_ge(S.r4, 1)
+    for e in range(EL):
+        V.tensor_scalar(T.st[:, 30 * e:30 * (e + 1)], T.ip[:, :], T.pcnt[:, e:e + 1], T.dl[:, e:e + 1], op.is_ge,
+                        op.mult).then_inc(S.r5, 1)
+    P.wait_ge(S.r5, 2)
+    P.matmul(T.prix[:, 0:60], T.rr[:, :], T.st[:, :], False, True).then_inc(S.m4, 1)
+    V.wait_ge(S.m4, 1)
+    V.tensor_copy(T.ro[:, :], T.prix[:, 0:60]).then_inc(S.r6, 1)
+
+    for e in (V, A):
+        e.wait_ge(S.r6, 1)
+        e.wait_ge(S.kz, 1)
+        e.wait_ge(S.gs3, 1)
+        e.wait_ge(S.data, data_total)
+    hc = HALF // 16
+    V.tensor_copy(T.y0[:, 0:HALF], T.land[:, :].indirect(T.ro[:, 0:hc])).then_inc(S.yva, 1)
+    V.tensor_copy(T.y0[:, HALF:CAP], T.land[:, :].indirect(T.ro[:, hc:30])).then_inc(S.yvb, 1)
+    cp = ActivationFunctionType.Copy
+    A.activation(T.y1[:, 0:HALF], T.land[:, :].indirect(T.ro[:, 30:30 + hc]), cp).then_inc(S.ysa, 1)
+    A.activation(T.y1[:, HALF:CAP], T.land[:, :].indirect(T.ro[:, 30 + hc:60]), cp).then_inc(S.ysb, 1)
+    for sem, src, a, b, o in ((S.yva, T.y0, 0, HALF, 0), (S.ysa, T.y1, 0, HALF, CAP), (S.yvb, T.y0, HALF, CAP, 0)):
+        Y.wait_ge(sem, 1)
+        Y.dma_start(T.y[:, o + a:o + b], src[:, a:b]).then_inc(S.sta, 16)
+    A.wait_ge(S.ysb, 1)
+    A.dma_start(T.y[:, CAP + HALF:2 * CAP], T.y1[:, HALF:CAP]).then_inc(S.stb, 16)
+    Y.wait_ge(S.sta, 48)
+    A.wait_ge(S.stb, 16)
+    g.wait_ge(S.loc, loc)

@@ -7,13 +7,15 @@ BLK = EL * CAPP
 ZC = CAPP + CAP
 LW = N * BLK + ZC
 HALF = 256
+BIG = 4096.0
+RND = 201326592.0
 
 SCRATCH = {
     "exall": ("dram", [N, 128, 8], "int32"),
     "xs": ("sbuf", [128, 1024], "float32"),
     "sb": ("sbuf", [128, N * BLK], "float32"),
     "land": ("sbuf", [128, LW], "float32"),
-    "rb": ("sbuf", [128, 2 * BLK], "float32"),
+    "rb": ("sbuf", [128, BLK], "float32"),
     "y0": ("sbuf", [128, CAP], "float32"),
     "y1": ("sbuf", [128, CAP], "float32"),
     "ext": ("sbuf", [128, 8], "int32"),
@@ -26,17 +28,20 @@ SCRATCH = {
     "pf": ("sbuf", [128, 4], "float32"),
     "sc": ("sbuf", [128, 4], "float32"),
     "wf": ("sbuf", [128, 128], "bfloat16"),
+    "chf": ("sbuf", [128, 128], "bfloat16"),
     "kf": ("sbuf", [128, 128], "bfloat16"),
+    "kf2": ("sbuf", [128, 128], "bfloat16"),
     "n16": ("sbuf", [128, 128], "bfloat16"),
-    "rf": ("sbuf", [128, 128], "bfloat16"),
+    "n16h": ("sbuf", [128, 128], "float16"),
     "c16": ("sbuf", [128, 60], "float32"),
     "ma": ("sbuf", [128, 128], "bfloat16"),
-    "mab": ("sbuf", [128, 128], "bfloat16"),
-    "mac": ("sbuf", [128, 128], "bfloat16"),
     "mb": ("sbuf", [128, 128], "bfloat16"),
-    "mc": ("sbuf", [128, 128], "bfloat16"),
+    "mc0": ("sbuf", [128, 128], "bfloat16"),
+    "i4": ("sbuf", [128, 128], "bfloat16"),
+    "mac": ("sbuf", [128, 128], "bfloat16"),
     "rst": ("sbuf", [128, 128], "float32"),
     "brow": ("sbuf", [128, 128], "bfloat16"),
+    "neg": ("sbuf", [128, 128], "bfloat16"),
     "ones": ("sbuf", [128, 128], "bfloat16"),
     "jc": ("sbuf", [128, 8], "float32"),
     "oh": ("sbuf", [128, 128], "bfloat16"),
@@ -44,15 +49,13 @@ SCRATCH = {
     "t2": ("sbuf", [128, 32], "bfloat16"),
     "t3": ("sbuf", [128, 16], "bfloat16"),
     "trep": ("sbuf", [128, 128], "bfloat16"),
-    "q": ("sbuf", [128, 128], "float32"),
     "vs": ("sbuf", [128, 128], "float32"),
-    "ni": ("sbuf", [128, 8], "int32"),
     "v16": ("sbuf", [128, 8], "float32"),
     "lh": ("sbuf", [128, 1024], "float16"),
     "rh": ("sbuf", [128, 1024], "float16"),
     "offs": ("sbuf", [128, 128], "uint16"),
     "le": ("sbuf", [128, 128], "bfloat16"),
-    "eq": ("sbuf", [128, 128], "bfloat16"),
+    "nl": ("sbuf", [128, 128], "bfloat16"),
     "rr": ("sbuf", [128, 128], "float16"),
     "bas": ("sbuf", [128, 60], "float16"),
     "ip": ("sbuf", [128, 30], "float32"),
@@ -68,8 +71,8 @@ SCRATCH = {
     "prix": ("psum", [128, 512], "float32"),
 }
 SEMAPHORES = (["meta", "data", "loc", "exs", "exd", "xl", "xal", "sta", "stb"]
-              + ["gi%d" % i for i in range(7)] + ["p1", "p2", "p3", "p4", "k1", "k3", "kz"]
-              + ["o1", "u1", "u2", "u3", "u4", "m1", "m2", "m3", "m4", "q1", "q2", "q3", "q4", "of"]
+              + ["gi%d" % i for i in range(7)] + ["p1", "p2", "p3", "p4", "p5", "k1", "k2", "k3", "kz"]
+              + ["o1", "u1", "u2", "u3", "u4", "m1", "m2", "m3", "m4", "q2", "q4", "of"]
               + ["b%d" % i for i in range(8)] + ["gv%d" % i for i in range(4)] + ["gs%d" % i for i in range(4)]
               + ["r1", "r2", "r3", "r4", "r5", "r6", "yva", "yvb", "ysa", "ysb"])
 
@@ -92,11 +95,13 @@ def routes(cores, topo):
     on = {x: [i for i, c in enumerate(cores) if topo.chip(c) == x] for x in chips}
     used = set(cores)
 
-    def relay(chip, die, dst):
-        h = [c for c in range(SIM) if topo.chip(c) == chip and topo.die(c) == die and c not in used
-             and topo.may_write(c, dst)][0]
-        used.add(h)
-        return h
+    def relays(chip, die, ranks):
+        found = []
+        for d in ranks:
+            found.append([c for c in range(SIM) if topo.chip(c) == chip and topo.die(c) == die and c not in used
+                          and topo.may_write(c, cores[d])][0])
+            used.add(found[-1])
+        return found
 
     plan = []
     for src in cores:
@@ -105,15 +110,14 @@ def routes(cores, topo):
         for x in chips:
             if x == cs:
                 continue
-            dst = cores[on[x][0]]
             rot = (chips.index(x) - chips.index(cs)) % len(chips)
             h = None
             if not topo.same_plane(cs, x):
                 if not topo.mates(cs, x) and mate[cs] in chips:
-                    h = relay(mate[x], topo.die(src), dst)
-                elif not topo.may_write(src, dst):
-                    h = relay(cs, topo.die(src), dst)
-            kind = 2 if h is None else (1 if topo.chip(h) == cs else 0)
+                    h = relays(mate[x], topo.die(src), on[x])
+                elif not topo.may_write(src, cores[on[x][0]]):
+                    h = relays(cs, topo.die(src), on[x])
+            kind = 2 if h is None else (1 if topo.chip(h[0]) == cs else 0)
             todo.append((kind, rot, on[x], h))
         todo.sort(key=lambda a: a[:2])
         plan.append([(a[2], a[3]) for a in todo])
@@ -132,27 +136,19 @@ def ident(topo, c):
     return DstId(rid=rid, pnc=pid)
 
 
-def pair(topo, src_aps, dst_aps, dsts, eng, sem):
-    h = len(eng) // 2
-    return [RemoteDMATransfer(dst_ids=[ident(topo, dsts[i])], dma_engine_mask=join(eng[i * h:(i + 1) * h]),
-                              remote_sem=sem, srcs=[src_aps[i]], dsts=[dst_aps[i]]) for i in range(2)]
-
-
 def cast(T, topo, r, dsts, eng):
     return RemoteDMATransfer(dst_ids=[ident(topo, d) for d in dsts], dma_engine_mask=join(eng), remote_sem=T.sem.meta,
                              srcs=[T.exall[r]], dsts=[T.exall[r] for d in dsts])
 
 
-def relay_program(g, core, T, topo, r, ranks):
-    cores = T.cores
+def relay_program(g, core, T, topo, r, d):
     off, near = masks(core, topo)
-    came = near if topo.chip(cores[r]) == topo.chip(core) else masks(cores[r], topo)[0]
-    dsts = [cores[d] for d in ranks]
+    came = near if topo.chip(T.cores[r]) == topo.chip(core) else masks(T.cores[r], topo)[0]
     g.wait_ge(T.sem.meta, len(came))
-    g.remote_dma_fused([cast(T, topo, r, dsts, off)], local_sem=T.sem.loc)
-    g.wait_ge(T.sem.data, len(came))
-    g.remote_dma_fused(pair(topo, [T.rb[:, i * BLK:(i + 1) * BLK] for i in range(2)],
-                            [T.land[:, r * BLK:(r + 1) * BLK]] * 2, dsts, off, T.sem.data), local_sem=T.sem.loc)
+    g.remote_dma_fused([cast(T, topo, r, [T.cores[d]], off)], local_sem=T.sem.loc)
+    g.wait_ge(T.sem.data, len(came) // 2)
+    rid, pid, _ = topo.addr(T.cores[d])
+    g.remote_dma(T.land[:, r * BLK:(r + 1) * BLK], T.rb[:, :], T.sem.data, T.sem.loc, pid, rid, join(off))
     g.wait_ge(T.sem.loc, 2 * len(off))
 
 
@@ -163,8 +159,8 @@ def rank_program(g, core, T, topo):
     if rank is None:
         for r in range(N):
             for ranks, h in plan[r]:
-                if h == core:
-                    relay_program(g, core, T, topo, r, ranks)
+                if h is not None and core in h:
+                    relay_program(g, core, T, topo, r, ranks[h.index(core)])
         return
     S = T.sem
     V, A, P, Y = g.vector, g.scalar, g.tensor, g.sync
@@ -177,9 +173,9 @@ def rank_program(g, core, T, topo):
     for r in range(N):
         for ranks, h in plan[r]:
             if rank in ranks:
-                eng = masks(h if h is not None else cores[r], topo)[0]
+                eng = masks(cores[r] if h is None else h[ranks.index(rank)], topo)[0]
                 meta_total += len(eng)
-                data_total += len(eng) // 2
+                data_total += len(eng) // 2 if h is None else len(eng)
 
     Y.dma_start(T.ext[:, :], T.ex[:, :]).then_inc(S.exs, 16)
     A.dma_start(T.exall[rank], T.ex[:, :]).then_inc(S.exd, 16)
@@ -188,36 +184,34 @@ def rank_program(g, core, T, topo):
     imp = {"allow_small_or_imprecise_dtypes": True}
     g.iota(T.pcol[:, :], [[0, 1]], 0, 1).then_inc(S.gi0, 1)
     g.iota(T.wf[:, :], [[1, 16], [16, 8]], 0, 0, **imp).then_inc(S.gi1, 1)
-    g.iota(T.ti[:, :], [[1, 8]], 0, 0).then_inc(S.gi2, 1)
-    g.iota(T.kf[:, :], [[0, 8], [1, 16]], 0, 0, **imp).then_inc(S.gi3, 1)
-    g.iota(T.n16[:, :], [[16, 128]], 16, 0, **imp).then_inc(S.gi4, 1)
-    g.iota(T.rf[:, :], [[1, 8], [0, 16]], 0, 0, **imp).then_inc(S.gi5, 1)
+    g.iota(T.chf[:, :], [[0, 16], [1, 8]], 0, 0, **imp).then_inc(S.gi2, 1)
+    g.iota(T.ti[:, :], [[1, 8]], 0, 0).then_inc(S.gi3, 1)
+    g.iota(T.kf[:, :], [[0, 8], [1, 16]], 0, 0, **imp).then_inc(S.gi4, 1)
+    g.iota(T.n16[:, :], [[16, 128]], 0, 0, **imp).then_inc(S.gi5, 1)
     g.iota(T.c16[:, :], [[128, 2], [16, 30]], 0, 0, **imp).then_inc(S.gi6, 1)
     out_, in_ = [], [cores[partner]]
     for ranks, h in mine:
         if h is None:
             out_ += [cores[d] for d in ranks]
-        elif topo.chip(h) == topo.chip(core):
-            in_.append(h)
+        elif topo.chip(h[0]) == topo.chip(core):
+            in_ += h
         else:
-            out_.append(h)
+            out_ += h
     g.wait_ge(S.exd, 16)
     g.remote_dma_fused([cast(T, topo, rank, out_, off), cast(T, topo, rank, in_, near)], local_sem=S.loc)
     loc = len(off) + len(near)
     for i, (ranks, h) in enumerate(mine):
         g.wait_ge(S["gv%d" % i], 1)
         g.wait_ge(S["gs%d" % i], 1)
-        a = ranks[0] * BLK
-        if h is None:
-            g.remote_dma_fused(pair(topo, [T.sb[:, d * BLK:(d + 1) * BLK] for d in ranks],
-                                    [T.land[:, rank * BLK:(rank + 1) * BLK]] * 2, [cores[d] for d in ranks], off, S.data),
-                               local_sem=S.loc)
-            loc += len(off)
-        else:
-            eng = near if topo.chip(h) == topo.chip(core) else off
-            rid, pid, _ = topo.addr(h)
-            g.remote_dma(T.rb[:, :], T.sb[:, a:a + 2 * BLK], S.data, S.loc, pid, rid, join(eng))
-            loc += len(eng)
+        eng = near if h is not None and topo.chip(h[0]) == topo.chip(core) else off
+        half = len(eng) // 2
+        to = [cores[d] for d in ranks] if h is None else h
+        g.remote_dma_fused([RemoteDMATransfer(
+            dst_ids=[ident(topo, to[b])], dma_engine_mask=join(eng[b * half:(b + 1) * half]), remote_sem=S.data,
+            srcs=[T.sb[:, d * BLK:(d + 1) * BLK]],
+            dsts=[T.land[:, rank * BLK:(rank + 1) * BLK] if h is None else T.rb[:, :]]) for b, d in enumerate(ranks)],
+            local_sem=S.loc)
+        loc += len(eng)
     g.wait_ge(S.gv3, 1)
     rid, pid, _ = topo.addr(cores[partner])
     g.remote_dma(T.land[:, rank * BLK:(rank + 1) * BLK], T.sb[:, partner * BLK:(partner + 1) * BLK], S.data, S.loc,
@@ -231,26 +225,24 @@ def rank_program(g, core, T, topo):
     V.wait_ge(S.p1, 4)
     V.tensor_copy(T.pf[:, :], T.pi[:, :]).then_inc(S.p2, 1)
     V.wait_ge(S.p2, 1)
-    V.tensor_scalar(T.sc[:, 0:1], T.pf[:, 0:1], 16.0, None, op.mult).then_inc(S.p3, 1)
-    V.tensor_scalar(T.sc[:, 1:2], T.pf[:, 0:1], 16.0, 15.0, op.mult, op.add).then_inc(S.p3, 1)
-    V.tensor_scalar(T.sc[:, 2:3], T.pf[:, 0:1], 16.0, T.pf[:, 1:2], op.mult, op.add).then_inc(S.p3, 1)
-    V.tensor_scalar(T.sc[:, 3:4], T.pf[:, 0:1], 128.0, T.pf[:, 1:2], op.mult, op.add).then_inc(S.p3, 1)
-    V.wait_ge(S.p3, 4)
+    V.tensor_scalar(T.sc[:, 0:1], T.pf[:, 0:1], 16.0, T.pf[:, 1:2], op.mult, op.add).then_inc(S.p3, 1)
+    V.tensor_scalar(T.sc[:, 1:2], T.pf[:, 0:1], 128.0, T.pf[:, 1:2], op.mult, op.add).then_inc(S.p3, 1)
+    V.wait_ge(S.p3, 2)
     V.wait_ge(S.gi1, 1)
-    V.tensor_scalar(T.ma[:, :], T.wf[:, :], T.sc[:, 1:2], None, op.is_gt).then_inc(S.p4, 1)
-    V.tensor_scalar(T.mab[:, :], T.wf[:, :], T.sc[:, 0:1], None, op.is_ge).then_inc(S.p4, 1)
-    V.tensor_scalar(T.mac[:, :], T.wf[:, :], T.sc[:, 2:3], None, op.is_gt).then_inc(S.p4, 1)
+    V.tensor_scalar(T.mc0[:, :], T.wf[:, :], T.sc[:, 0:1], None, op.is_gt).then_inc(S.p4, 1)
+    V.tensor_scalar(T.i4[:, :], T.wf[:, :], T.sc[:, 0:1], BIG, op.is_equal, op.mult).then_inc(S.p4, 1)
     V.wait_ge(S.gi2, 1)
+    V.tensor_scalar(T.ma[:, :], T.chf[:, :], T.pf[:, 0:1], None, op.is_gt).then_inc(S.k1, 1)
+    V.tensor_scalar(T.mb[:, :], T.chf[:, :], T.pf[:, 0:1], None, op.is_equal).then_inc(S.k1, 1)
+    V.wait_ge(S.gi3, 1)
     V.tensor_copy(T.tu[:, :], T.ti[:, :]).then_inc(S.k1, 1)
     V.tensor_scalar(T.mu[:, :], T.ti[:, :], 0.0, T.pf[:, 2:3], op.mult, op.add).then_inc(S.k1, 1)
-    V.tensor_scalar(T.jc[:, :], T.ti[:, :], 16.0, T.sc[:, 3:4], op.mult, op.add).then_inc(S.k1, 1)
-    V.wait_ge(S.p4, 3)
-    V.tensor_tensor(T.mb[:, :], T.mab[:, :], T.ma[:, :], op.subtract).then_inc(S.k1, 1)
-    V.tensor_tensor(T.mc[:, :], T.mac[:, :], T.ma[:, :], op.subtract).then_inc(S.k1, 1)
     V.memset(T.ones[:, :], 1.0).then_inc(S.k1, 1)
-    V.wait_ge(S.gi3, 1)
-    V.tensor_scalar(T.rst[:, :], T.kf[:, :], 0.0, None, op.is_gt).then_inc(S.k1, 1)
-    V.tensor_scalar(T.brow[:, :], T.kf[:, :], 128.0, 16.0, op.mult, op.add).then_inc(S.k1, 1)
+    V.memset(T.neg[:, :], -7.5).then_inc(S.k1, 1)
+    V.wait_ge(S.p4, 2)
+    V.tensor_tensor(T.mac[:, :], T.mc0[:, :], T.i4[:, :], op.add).then_inc(S.k1, 1)
+    V.wait_ge(S.gi4, 1)
+    V.tensor_scalar(T.brow[:, :], T.kf[:, :], 128.0, None, op.mult).then_inc(S.k1, 1)
     K1 = 8
     V.wait_ge(S.k1, K1)
     V.wait_ge(S.exs, 16)
@@ -262,31 +254,32 @@ def rank_program(g, core, T, topo):
     V.wait_ge(S.u2, 1)
     V.tensor_tensor(T.t3[:, :], T.t2[:, 0:16], T.t2[:, 16:32], op.add).then_inc(S.u3, 1)
     V.wait_ge(S.u3, 1)
-    V.tensor_copy(T.trep[:, :], T.t3[:, 0:16].indirect(T.mu[:, 0:8])).then_inc(S.u4, 1)
+    V.tensor_tensor(T.trep[:, :], T.t3[:, 0:16].indirect(T.mu[:, 0:8]), T.oh[:, :], op.subtract).then_inc(S.u4, 1)
+    V.tensor_scalar(T.rst[:, :], T.kf[:, :], 0.0, None, op.is_gt).then_inc(S.k2, 1)
+    V.tensor_scalar(T.kf2[:, :], T.kf[:, :], -7.5, None, op.add).then_inc(S.k2, 1)
+    V.tensor_scalar(T.jc[:, :], T.ti[:, :], 16.0, T.sc[:, 1:2], op.mult, op.add).then_inc(S.k2, 1)
+    V.wait_ge(S.gi5, 1)
+    V.tensor_scalar(T.n16h[:, :], T.n16[:, :], BIG, None, op.add).then_inc(S.k2, 1)
+    V.wait_ge(S.k2, 4)
     V.wait_ge(S.m1, 1)
-    V.tensor_tensor(T.q[:, :], T.oh[:, :], T.pcum[:, 0:128], op.mult).then_inc(S.q1, 1)
-    V.wait_ge(S.q1, 1)
-    V.tensor_tensor_scan(T.vs[:, :], T.rst[:, :], T.q[:, :], 0.0, op.mult, op.add).then_inc(S.q2, 1)
+    V.tensor_tensor_scan(T.vs[:, :], T.rst[:, :], T.pcum[:, 0:128], 0.0, op.mult, op.max).then_inc(S.q2, 1)
     V.wait_ge(S.q2, 1)
-    V.tensor_scalar(T.ni[:, :], T.vs[:, 15::16], 0.0625, -0.46875, op.mult, op.add).then_inc(S.q3, 1)
-    V.wait_ge(S.q3, 1)
-    V.tensor_scalar(T.v16[:, :], T.ni[:, :], 16.0, None, op.mult).then_inc(S.q4, 1)
-    V.wait_ge(S.gi4, 1)
+    V.tensor_scalar(T.v16[:, :], T.vs[:, 15::16], RND, RND, op.add, op.subtract).then_inc(S.q4, 1)
     V.wait_ge(S.q4, 1)
     for t in range(8):
         c = slice(128 * t, 128 * (t + 1))
-        V.tensor_scalar(T.lh[:, c], T.kf[:, :], T.v16[:, t:t + 1], T.vs[:, 16 * t + 15:16 * t + 16], op.add,
+        V.tensor_scalar(T.lh[:, c], T.kf2[:, :], T.v16[:, t:t + 1], T.vs[:, 16 * t + 15:16 * t + 16], op.add,
                         op.is_equal).then_inc(S["b%d" % t], 1)
-        V.tensor_scalar(T.rh[:, c], T.n16[:, :], T.v16[:, t:t + 1], T.jc[:, t:t + 1], op.is_equal,
+        V.tensor_scalar(T.rh[:, c], T.n16h[:, :], T.v16[:, t:t + 1], T.jc[:, t:t + 1], op.is_equal,
                         op.mult).then_inc(S["b%d" % t], 1)
     V.wait_ge(S.m2, 1)
     V.tensor_copy(T.offs[:, :], T.pidx[:, 0:128]).then_inc(S.of, 1)
 
-    P.wait_ge(S.p4, 3)
     P.wait_ge(S.k1, K1)
     P.matmul(T.pcum[:, 0:128], T.ones[0:1, :], T.brow[0:1, :], True, False)
+    P.matmul(T.pcum[:, 0:128], T.ones[0:1, :], T.neg[0:1, :], False, False)
     P.wait_ge(S.o1, 1)
-    P.matmul(T.pcum[:, 0:128], T.mc[:, :], T.oh[:, :], False, False)
+    P.matmul(T.pcum[:, 0:128], T.mac[:, :], T.oh[:, :], False, False)
     for d in range(1, 8):
         P.matmul(T.pcum[:, 16 * d:128], T.mb[:, :], T.oh[:, 0:128 - 16 * d], False, False)
     P.wait_ge(S.u4, 1)
@@ -297,12 +290,14 @@ def rank_program(g, core, T, topo):
         m = P.matmul(T.pidx[:, 0:128], T.lh[:, c], T.rh[:, c], t == 0, t == 7)
     m.then_inc(S.m2, 1)
 
+    cp = ActivationFunctionType.Copy
+
     def pack(eng, d, out, sem):
         src = T.xs[:, 0:1024].indirect(T.offs[:, 16 * d:16 * (d + 1)])
         if eng == "v":
             V.tensor_copy(out, src).then_inc(sem, 1)
         else:
-            A.activation(out, src, ActivationFunctionType.Copy).then_inc(sem, 1)
+            A.activation(out, src, cp, bias=-0.0).then_inc(sem, 1)
 
     for e in (V, A):
         e.wait_ge(S.of, 1)
@@ -318,10 +313,12 @@ def rank_program(g, core, T, topo):
     Y.wait_ge(S.meta, meta_total)
     Y.dma_start(T.xa[:, :], T.exall[:, :, :]).then_inc(S.xal, 16)
     V.memset(T.land[:, N * BLK:LW], 0.0).then_inc(S.kz, 1)
-    V.wait_ge(S.gi5, 1)
+    V.tensor_scalar(T.sc[:, 2:3], T.pf[:, 3:4], 256.0, None, op.mult).then_inc(S.p5, 1)
+    V.tensor_scalar(T.sc[:, 3:4], T.pf[:, 3:4], 256.0, 256.0, op.mult, op.add).then_inc(S.p5, 1)
+    V.wait_ge(S.p5, 2)
     V.wait_ge(S.gi6, 1)
-    V.tensor_scalar(T.le[:, :], T.rf[:, :], T.pf[:, 3:4], None, op.is_ge).then_inc(S.k3, 1)
-    V.tensor_scalar(T.eq[:, :], T.rf[:, :], T.pf[:, 3:4], None, op.is_equal).then_inc(S.k3, 1)
+    V.tensor_scalar(T.le[:, :], T.n16[:, :], T.sc[:, 2:3], None, op.is_ge).then_inc(S.k3, 1)
+    V.tensor_scalar(T.nl[:, :], T.n16[:, :], T.sc[:, 3:4], -1.0, op.is_ge, op.mult).then_inc(S.k3, 1)
     V.tensor_scalar(T.rr[:, :], T.kf[:, :], T.pf[:, 2:3], None, op.is_equal).then_inc(S.k3, 1)
     V.tensor_scalar(T.bas[:, :], T.c16[:, :], T.pf[:, 2:3], None, op.add).then_inc(S.k3, 1)
     V.tensor_scalar(T.ip[:, :], T.c16[:, 0:30], T.pf[:, 2:3], None, op.add).then_inc(S.k3, 1)
@@ -338,7 +335,8 @@ def rank_program(g, core, T, topo):
     P.matmul(T.prix[:, 0:60], T.rr[0:16, :], T.bas[0:16, :], True, False)
     P.wait_ge(S.r3, 1)
     P.matmul(T.pcnt[:, 0:2], T.le[:, :], T.cnb[:, :], True, True)
-    P.matmul(T.pcnt[:, 2:4], T.eq[:, :], T.cnb[:, :], True, True).then_inc(S.m3, 1)
+    P.matmul(T.pcnt[:, 2:4], T.le[:, :], T.cnb[:, :], True, False)
+    P.matmul(T.pcnt[:, 2:4], T.nl[:, :], T.cnb[:, :], False, True).then_inc(S.m3, 1)
     V.wait_ge(S.k3, 5)
     V.wait_ge(S.m3, 1)
     V.tensor_scalar(T.dl[:, :], T.pcnt[:, 2:4], -1.0, float(BLK), op.mult, op.add).then_inc(S.r4, 1)
@@ -359,9 +357,8 @@ def rank_program(g, core, T, topo):
     hc = HALF // 16
     V.tensor_copy(T.y0[:, 0:HALF], T.land[:, :].indirect(T.ro[:, 0:hc])).then_inc(S.yva, 1)
     V.tensor_copy(T.y0[:, HALF:CAP], T.land[:, :].indirect(T.ro[:, hc:30])).then_inc(S.yvb, 1)
-    cp = ActivationFunctionType.Copy
-    A.activation(T.y1[:, 0:HALF], T.land[:, :].indirect(T.ro[:, 30:30 + hc]), cp).then_inc(S.ysa, 1)
-    A.activation(T.y1[:, HALF:CAP], T.land[:, :].indirect(T.ro[:, 30 + hc:60]), cp).then_inc(S.ysb, 1)
+    A.activation(T.y1[:, 0:HALF], T.land[:, :].indirect(T.ro[:, 30:30 + hc]), cp, bias=-0.0).then_inc(S.ysa, 1)
+    A.activation(T.y1[:, HALF:CAP], T.land[:, :].indirect(T.ro[:, 30 + hc:60]), cp, bias=-0.0).then_inc(S.ysb, 1)
     for sem, src, a, b, o in ((S.yva, T.y0, 0, HALF, 0), (S.ysa, T.y1, 0, HALF, CAP), (S.yvb, T.y0, HALF, CAP, 0)):
         Y.wait_ge(sem, 1)
         Y.dma_start(T.y[:, o + a:o + b], src[:, a:b]).then_inc(S.sta, 16)

@@ -11,70 +11,68 @@ BIG = 4096.0
 RND = 201326592.0
 
 SCRATCH = {
-    "exall": ("dram", [N, 128, 8], "int32"),
     "xs": ("sbuf", [128, 1024], "float32"),
     "sb": ("sbuf", [128, N * BLK], "float32"),
     "land": ("sbuf", [128, LW], "float32"),
-    "rb": ("sbuf", [128, BLK], "float32"),
+    "rb": ("sbuf", [128, 2 * BLK], "float32"),
     "y0": ("sbuf", [128, CAP], "float32"),
     "y1": ("sbuf", [128, CAP], "float32"),
-    "ext": ("sbuf", [128, 8], "int32"),
-    "xa": ("sbuf", [128, 64], "int32"),
+    "xa": ("sbuf", [128, N * 8], "int32"),
     "pcol": ("sbuf", [128, 1], "int32"),
     "ti": ("sbuf", [128, 8], "int32"),
     "tu": ("sbuf", [128, 8], "uint16"),
-    "mu": ("sbuf", [128, 8], "uint16"),
-    "pi": ("sbuf", [128, 4], "int32"),
+    "pi": ("sbuf", [128, 3], "int32"),
     "pf": ("sbuf", [128, 4], "float32"),
     "sc": ("sbuf", [128, 4], "float32"),
-    "wf": ("sbuf", [128, 128], "bfloat16"),
+    "cf": ("sbuf", [128, 128], "bfloat16"),
     "chf": ("sbuf", [128, 128], "bfloat16"),
     "kf": ("sbuf", [128, 128], "bfloat16"),
     "kf2": ("sbuf", [128, 128], "bfloat16"),
-    "n16": ("sbuf", [128, 128], "bfloat16"),
     "n16h": ("sbuf", [128, 128], "float16"),
     "c16": ("sbuf", [128, 60], "float32"),
     "ma": ("sbuf", [128, 128], "bfloat16"),
     "mb": ("sbuf", [128, 128], "bfloat16"),
-    "mc0": ("sbuf", [128, 128], "bfloat16"),
+    "gt": ("sbuf", [128, 128], "bfloat16"),
     "i4": ("sbuf", [128, 128], "bfloat16"),
-    "mac": ("sbuf", [128, 128], "bfloat16"),
+    "mx": ("sbuf", [128, 128], "bfloat16"),
+    "s1": ("sbuf", [128, 128], "bfloat16"),
+    "s2": ("sbuf", [128, 128], "bfloat16"),
+    "x1": ("sbuf", [128, 128], "bfloat16"),
+    "x2": ("sbuf", [128, 128], "bfloat16"),
     "rst": ("sbuf", [128, 128], "float32"),
     "brow": ("sbuf", [128, 128], "bfloat16"),
     "neg": ("sbuf", [128, 128], "bfloat16"),
     "ones": ("sbuf", [128, 128], "bfloat16"),
+    "c256": ("sbuf", [128, 2], "bfloat16"),
     "jc": ("sbuf", [128, 8], "float32"),
     "oh": ("sbuf", [128, 128], "bfloat16"),
-    "t1": ("sbuf", [128, 64], "bfloat16"),
-    "t2": ("sbuf", [128, 32], "bfloat16"),
-    "t3": ("sbuf", [128, 16], "bfloat16"),
-    "trep": ("sbuf", [128, 128], "bfloat16"),
     "vs": ("sbuf", [128, 128], "float32"),
     "v16": ("sbuf", [128, 8], "float32"),
     "lh": ("sbuf", [128, 1024], "float16"),
     "rh": ("sbuf", [128, 1024], "float16"),
     "offs": ("sbuf", [128, 128], "uint16"),
     "le": ("sbuf", [128, 128], "bfloat16"),
-    "nl": ("sbuf", [128, 128], "bfloat16"),
+    "nle": ("sbuf", [128, 128], "bfloat16"),
+    "lt": ("sbuf", [128, 128], "bfloat16"),
     "rr": ("sbuf", [128, 128], "float16"),
     "bas": ("sbuf", [128, 60], "float16"),
     "ip": ("sbuf", [128, 30], "float32"),
-    "eqx": ("sbuf", [128, 128], "float32"),
-    "cnf": ("sbuf", [128, 2], "float32"),
+    "eqx": ("sbuf", [128, 128], "bfloat16"),
     "cnb": ("sbuf", [128, 2], "bfloat16"),
-    "dl": ("sbuf", [128, 2], "float32"),
     "st": ("sbuf", [128, 60], "float16"),
     "ro": ("sbuf", [128, 60], "uint16"),
+    "px1": ("psum", [128, 512], "float32"),
+    "px2": ("psum", [128, 512], "float32"),
     "pcum": ("psum", [128, 512], "float32"),
     "pidx": ("psum", [128, 512], "float32"),
     "pcnt": ("psum", [128, 512], "float32"),
     "prix": ("psum", [128, 512], "float32"),
 }
-SEMAPHORES = (["meta", "data", "loc", "exs", "exd", "xl", "xal", "sta", "stb"]
-              + ["gi%d" % i for i in range(7)] + ["p1", "p2", "p3", "p4", "p5", "k1", "k2", "k3", "kz"]
-              + ["o1", "u1", "u2", "u3", "u4", "m1", "m2", "m3", "m4", "q2", "q4", "of"]
-              + ["b%d" % i for i in range(8)] + ["gv%d" % i for i in range(4)] + ["gs%d" % i for i in range(4)]
-              + ["r1", "r2", "r3", "r4", "r5", "r6", "yva", "yvb", "ysa", "ysb"])
+SEMAPHORES = (["meta", "data", "rb0", "rb1", "loc", "exs", "xl", "sta"]
+              + ["gi%d" % i for i in range(6)] + ["p1", "p2", "p5", "k0", "k1", "k2", "k3", "k4", "k5", "k6", "k7", "kz"]
+              + ["o1", "h1", "h2", "w1", "w2", "m1", "m2", "m3", "m4", "q2", "q4", "of"]
+              + ["b%d" % i for i in range(8)] + ["pk%d" % i for i in range(7)] + ["own"]
+              + ["r1", "r2", "r3", "r5", "r6", "yv0", "yv1", "ys0", "ys1"])
 
 
 def bits(m):
@@ -96,32 +94,43 @@ def routes(cores, topo):
     used = set(cores)
 
     def relays(chip, die, ranks):
-        found = []
-        for d in ranks:
-            found.append([c for c in range(SIM) if topo.chip(c) == chip and topo.die(c) == die and c not in used
-                          and topo.may_write(c, cores[d])][0])
-            used.add(found[-1])
+        found = [c for c in range(SIM) if topo.chip(c) == chip and topo.die(c) == die and c not in used
+                 and all(topo.may_write(c, cores[d]) for d in ranks)]
+        found = [found[min(i, len(found) - 1)] for i in range(len(ranks))]
+        used.update(found)
         return found
 
     plan = []
     for src in cores:
-        cs = topo.chip(src)
-        todo = []
-        for x in chips:
-            if x == cs:
-                continue
-            rot = (chips.index(x) - chips.index(cs)) % len(chips)
-            h = None
-            if not topo.same_plane(cs, x):
-                if not topo.mates(cs, x) and mate[cs] in chips:
-                    h = relays(mate[x], topo.die(src), on[x])
-                elif not topo.may_write(src, cores[on[x][0]]):
-                    h = relays(cs, topo.die(src), on[x])
-            kind = 2 if h is None else (1 if topo.chip(h[0]) == cs else 0)
-            todo.append((kind, rot, on[x], h))
-        todo.sort(key=lambda a: a[:2])
-        plan.append([(a[2], a[3]) for a in todo])
+        cs, die = topo.chip(src), topo.die(src)
+        others = sorted((x for x in chips if x != cs), key=lambda x: (chips.index(x) - chips.index(cs)) % len(chips))
+        far = [x for x in others if not topo.same_plane(cs, x) and not topo.mates(cs, x)]
+        barred = [x for x in others if not topo.may_write(src, cores[on[x][0]])]
+        if mate[cs] in chips and far:
+            m = on[mate[cs]]
+            (a0, a1), (b0, b1) = [on[x] for x in far]
+            ra, rb = [relays(mate[x], die, on[x][:1])[0] for x in far]
+            h0, h1 = relays(cs, die, m)
+            if barred:
+                away = [(a0, ra), (b0, rb), (a1, relays(mate[far[0]], die, [a1])[0])]
+                here = [(b1, h1), (m[0], h0), (m[1], h0)]
+            else:
+                away = [(a0, ra), (b0, rb), (b1, None), (a1, None)]
+                here = [(m[0], h0), (m[1], h1)]
+        else:
+            hand = (barred or [x for x in others if topo.same_plane(cs, x)])[-1]
+            here = list(zip(on[hand], relays(cs, die, on[hand])))
+            away = [(d, None) for x in others if x != hand for d in on[x]]
+        plan.append([[away[0]], [here[0]], [away[1], here[1]], away[2:] + here[2:]])
     return plan
+
+
+def jobs_of(plan, core):
+    for r, calls in enumerate(plan):
+        mine = [d for call in calls for d, h in call if h == core]
+        if mine:
+            return r, mine
+    return None, []
 
 
 def masks(core, topo):
@@ -131,25 +140,42 @@ def masks(core, topo):
     return off, [i for i in bits(topo.mask(core, near)) if i not in off]
 
 
+def engines(core, to, topo):
+    off, near = masks(core, topo)
+    res = []
+    for i, c in enumerate(to):
+        here = topo.chip(c) == topo.chip(core)
+        same = [j for j, b in enumerate(to) if (topo.chip(b) == topo.chip(core)) == here]
+        e = near if here else off
+        w = len(e) // len(same)
+        res.append(e[same.index(i) * w:(same.index(i) + 1) * w])
+    return res
+
+
 def ident(topo, c):
     rid, pid, _ = topo.addr(c)
     return DstId(rid=rid, pnc=pid)
 
 
 def cast(T, topo, r, dsts, eng):
+    at = T.xa[:, 8 * r:8 * r + 8]
     return RemoteDMATransfer(dst_ids=[ident(topo, d) for d in dsts], dma_engine_mask=join(eng), remote_sem=T.sem.meta,
-                             srcs=[T.exall[r]], dsts=[T.exall[r] for d in dsts])
+                             srcs=[at], dsts=[at for d in dsts])
 
 
-def relay_program(g, core, T, topo, r, d):
-    off, near = masks(core, topo)
-    came = near if topo.chip(T.cores[r]) == topo.chip(core) else masks(T.cores[r], topo)[0]
-    g.wait_ge(T.sem.meta, len(came))
-    g.remote_dma_fused([cast(T, topo, r, [T.cores[d]], off)], local_sem=T.sem.loc)
-    g.wait_ge(T.sem.data, len(came) // 2)
-    rid, pid, _ = topo.addr(T.cores[d])
-    g.remote_dma(T.land[:, r * BLK:(r + 1) * BLK], T.rb[:, :], T.sem.data, T.sem.loc, pid, rid, join(off))
-    g.wait_ge(T.sem.loc, 2 * len(off))
+def relay_program(g, core, T, topo, plan, r, ds):
+    off = masks(core, topo)[0]
+    src = T.cores[r]
+    g.wait_ge(T.sem.meta, len(engines(src, [core], topo)[0]))
+    g.remote_dma_fused([cast(T, topo, r, [T.cores[d] for d in ds], off)], local_sem=T.sem.loc)
+    for i, d in enumerate(ds):
+        call = [c for c in plan[r] if (d, core) in c][0]
+        eng = engines(src, [T.cores[b] if h is None else h for b, h in call], topo)[call.index((d, core))]
+        g.wait_ge(T.sem["rb%d" % i], len(eng))
+        rid, pid, _ = topo.addr(T.cores[d])
+        g.remote_dma(T.land[:, r * BLK:(r + 1) * BLK], T.rb[:, i * BLK:(i + 1) * BLK], T.sem.data, T.sem.loc, pid, rid,
+                     join(off))
+    g.wait_ge(T.sem.loc, (1 + len(ds)) * len(off))
 
 
 def rank_program(g, core, T, topo):
@@ -157,10 +183,9 @@ def rank_program(g, core, T, topo):
     plan = routes(cores, topo)
     rank = T.rank_of(core)
     if rank is None:
-        for r in range(N):
-            for ranks, h in plan[r]:
-                if h is not None and core in h:
-                    relay_program(g, core, T, topo, r, ranks[h.index(core)])
+        r, ds = jobs_of(plan, core)
+        if ds:
+            relay_program(g, core, T, topo, plan, r, ds)
         return
     S = T.sem
     V, A, P, Y = g.vector, g.scalar, g.tensor, g.sync
@@ -171,95 +196,91 @@ def rank_program(g, core, T, topo):
     meta_total = len(near)
     data_total = len(near)
     for r in range(N):
-        for ranks, h in plan[r]:
-            if rank in ranks:
-                eng = masks(cores[r] if h is None else h[ranks.index(rank)], topo)[0]
-                meta_total += len(eng)
-                data_total += len(eng) // 2 if h is None else len(eng)
+        for call in plan[r]:
+            to = [cores[d] if h is None else h for d, h in call]
+            for (d, h), e in zip(call, engines(cores[r], to, topo)):
+                if d == rank:
+                    full = masks(cores[r] if h is None else h, topo)[0]
+                    meta_total += len(full)
+                    data_total += len(e) if h is None else len(full)
 
-    Y.dma_start(T.ext[:, :], T.ex[:, :]).then_inc(S.exs, 16)
-    A.dma_start(T.exall[rank], T.ex[:, :]).then_inc(S.exd, 16)
+    ext = T.xa[:, 8 * rank:8 * rank + 8]
+    Y.dma_start(ext, T.ex[:, :]).then_inc(S.exs, 16)
     Y.dma_start(T.xs[:, :], T.x[:, :]).then_inc(S.xl, 16)
 
     imp = {"allow_small_or_imprecise_dtypes": True}
     g.iota(T.pcol[:, :], [[0, 1]], 0, 1).then_inc(S.gi0, 1)
-    g.iota(T.wf[:, :], [[1, 16], [16, 8]], 0, 0, **imp).then_inc(S.gi1, 1)
-    g.iota(T.chf[:, :], [[0, 16], [1, 8]], 0, 0, **imp).then_inc(S.gi2, 1)
-    g.iota(T.ti[:, :], [[1, 8]], 0, 0).then_inc(S.gi3, 1)
-    g.iota(T.kf[:, :], [[0, 8], [1, 16]], 0, 0, **imp).then_inc(S.gi4, 1)
-    g.iota(T.n16[:, :], [[16, 128]], 0, 0, **imp).then_inc(S.gi5, 1)
-    g.iota(T.c16[:, :], [[128, 2], [16, 30]], 0, 0, **imp).then_inc(S.gi6, 1)
-    out_, in_ = [], [cores[partner]]
-    for ranks, h in mine:
-        if h is None:
-            out_ += [cores[d] for d in ranks]
-        elif topo.chip(h[0]) == topo.chip(core):
-            in_ += h
-        else:
-            out_ += h
-    g.wait_ge(S.exd, 16)
+    g.iota(T.kf[:, :], [[0, 8], [1, 16]], 0, 0, **imp).then_inc(S.gi1, 1)
+    g.iota(T.ti[:, :], [[1, 8]], 0, 0).then_inc(S.gi2, 1)
+    g.iota(T.chf[:, :], [[0, 16], [1, 8]], 0, 0, **imp).then_inc(S.gi3, 1)
+    g.iota(T.cf[:, :], [[1, 128]], 0, 0, **imp).then_inc(S.gi4, 1)
+    targets = [cores[d] if h is None else h for call in mine for d, h in call]
+    out_ = sorted({t for t in targets if topo.chip(t) != topo.chip(core)})
+    in_ = sorted({t for t in targets if topo.chip(t) == topo.chip(core)}) + [cores[partner]]
+    g.wait_ge(S.exs, 16)
     g.remote_dma_fused([cast(T, topo, rank, out_, off), cast(T, topo, rank, in_, near)], local_sem=S.loc)
     loc = len(off) + len(near)
-    for i, (ranks, h) in enumerate(mine):
-        g.wait_ge(S["gv%d" % i], 1)
-        g.wait_ge(S["gs%d" % i], 1)
-        eng = near if h is not None and topo.chip(h[0]) == topo.chip(core) else off
-        half = len(eng) // 2
-        to = [cores[d] for d in ranks] if h is None else h
-        g.remote_dma_fused([RemoteDMATransfer(
-            dst_ids=[ident(topo, to[b])], dma_engine_mask=join(eng[b * half:(b + 1) * half]), remote_sem=S.data,
-            srcs=[T.sb[:, d * BLK:(d + 1) * BLK]],
-            dsts=[T.land[:, rank * BLK:(rank + 1) * BLK] if h is None else T.rb[:, :]]) for b, d in enumerate(ranks)],
-            local_sem=S.loc)
-        loc += len(eng)
-    g.wait_ge(S.gv3, 1)
+    g.iota(T.c16[:, :], [[128, 2], [16, 30]], 0, 0, **imp).then_inc(S.gi5, 1)
+    n = 0
+    for call in mine:
+        tr = []
+        to = [cores[d] if h is None else h for d, h in call]
+        for (d, h), c, eng in zip(call, to, engines(core, to, topo)):
+            g.wait_ge(S["pk%d" % n], 2 if n < 2 else 1)
+            n += 1
+            if h is None:
+                sem, dst = S.data, T.land[:, rank * BLK:(rank + 1) * BLK]
+            else:
+                k = jobs_of(plan, h)[1].index(d)
+                sem, dst = S["rb%d" % k], T.rb[:, k * BLK:(k + 1) * BLK]
+            tr.append(RemoteDMATransfer(dst_ids=[ident(topo, c)], dma_engine_mask=join(eng), remote_sem=sem,
+                                        srcs=[T.sb[:, d * BLK:(d + 1) * BLK]], dsts=[dst]))
+            loc += len(eng)
+        g.remote_dma_fused(tr, local_sem=S.loc)
+    g.wait_ge(S.pk6, 1)
     rid, pid, _ = topo.addr(cores[partner])
     g.remote_dma(T.land[:, rank * BLK:(rank + 1) * BLK], T.sb[:, partner * BLK:(partner + 1) * BLK], S.data, S.loc,
                  pid, rid, join(near))
     loc += len(near)
 
+    cp = ActivationFunctionType.Copy
+    A.wait_ge(S.gi1, 1)
+    A.activation(T.ones[:, :], T.kf[:, :], cp, bias=1.0, scale=0.0).then_inc(S.k0, 1)
+    A.activation(T.brow[:, :], T.kf[:, :], cp, scale=128.0).then_inc(S.k0, 1)
+    A.activation(T.neg[:, :], T.kf[:, :], cp, bias=-7.5, scale=0.0).then_inc(S.k0, 1)
+    A.activation(T.c256[:, :], T.kf[:, 0:2], cp, bias=float(BLK), scale=0.0).then_inc(S.k0, 1)
+
     V.wait_ge(S.gi0, 1)
-    for i, (o, n) in enumerate([(op.bitwise_and, 7), (op.logical_shift_right, 3), (op.bitwise_and, 15),
-                                (op.logical_shift_right, 4)]):
-        V.tensor_scalar(T.pi[:, i:i + 1], T.pcol[:, :], n, None, o).then_inc(S.p1, 1)
-    V.wait_ge(S.p1, 4)
-    V.tensor_copy(T.pf[:, :], T.pi[:, :]).then_inc(S.p2, 1)
-    V.wait_ge(S.p2, 1)
-    V.tensor_scalar(T.sc[:, 0:1], T.pf[:, 0:1], 16.0, T.pf[:, 1:2], op.mult, op.add).then_inc(S.p3, 1)
-    V.tensor_scalar(T.sc[:, 1:2], T.pf[:, 0:1], 128.0, T.pf[:, 1:2], op.mult, op.add).then_inc(S.p3, 1)
-    V.wait_ge(S.p3, 2)
-    V.wait_ge(S.gi1, 1)
-    V.tensor_scalar(T.mc0[:, :], T.wf[:, :], T.sc[:, 0:1], None, op.is_gt).then_inc(S.p4, 1)
-    V.tensor_scalar(T.i4[:, :], T.wf[:, :], T.sc[:, 0:1], BIG, op.is_equal, op.mult).then_inc(S.p4, 1)
+    for i, (o, c) in enumerate([(op.bitwise_and, 7), (op.logical_shift_right, 3), (op.bitwise_and, 15)]):
+        V.tensor_scalar(T.pi[:, i:i + 1], T.pcol[:, :], c, None, o).then_inc(S.p1, 1)
+    V.tensor_copy(T.pf[:, 3:4], T.pcol[:, :]).then_inc(S.p2, 1)
+    V.wait_ge(S.p1, 3)
+    V.tensor_copy(T.pf[:, 0:3], T.pi[:, :]).then_inc(S.p2, 1)
     V.wait_ge(S.gi2, 1)
+    V.tensor_copy(T.tu[:, :], T.ti[:, :]).then_inc(S.k1, 1)
+    V.wait_ge(S.p2, 2)
+    V.wait_ge(S.gi1, 1)
+    V.tensor_scalar(T.s1[:, :], T.kf[:, :], T.pf[:, 2:3], None, op.is_equal).then_inc(S.k4, 1)
+    V.wait_ge(S.gi3, 1)
     V.tensor_scalar(T.ma[:, :], T.chf[:, :], T.pf[:, 0:1], None, op.is_gt).then_inc(S.k1, 1)
     V.tensor_scalar(T.mb[:, :], T.chf[:, :], T.pf[:, 0:1], None, op.is_equal).then_inc(S.k1, 1)
-    V.wait_ge(S.gi3, 1)
-    V.tensor_copy(T.tu[:, :], T.ti[:, :]).then_inc(S.k1, 1)
-    V.tensor_scalar(T.mu[:, :], T.ti[:, :], 0.0, T.pf[:, 2:3], op.mult, op.add).then_inc(S.k1, 1)
-    V.memset(T.ones[:, :], 1.0).then_inc(S.k1, 1)
-    V.memset(T.neg[:, :], -7.5).then_inc(S.k1, 1)
-    V.wait_ge(S.p4, 2)
-    V.tensor_tensor(T.mac[:, :], T.mc0[:, :], T.i4[:, :], op.add).then_inc(S.k1, 1)
     V.wait_ge(S.gi4, 1)
-    V.tensor_scalar(T.brow[:, :], T.kf[:, :], 128.0, None, op.mult).then_inc(S.k1, 1)
-    K1 = 8
-    V.wait_ge(S.k1, K1)
+    V.tensor_scalar(T.gt[:, :], T.cf[:, :], T.pf[:, 3:4], None, op.is_gt).then_inc(S.k4, 1)
+    V.tensor_scalar(T.i4[:, :], T.cf[:, :], T.pf[:, 3:4], BIG, op.is_equal, op.mult).then_inc(S.k5, 1)
+    V.wait_ge(S.k1, 3)
     V.wait_ge(S.exs, 16)
-    V.tensor_tensor(T.oh[:, :], T.ext[:, 0:8].indirect(T.tu[:, 0:8]), T.kf[:, :], op.is_equal).then_inc(S.o1, 1)
-    V.wait_ge(S.o1, 1)
-    V.tensor_tensor(T.t1[:, :], T.oh[:, 0:64], T.oh[:, 64:128], op.add).then_inc(S.u1, 1)
-    V.wait_ge(S.u1, 1)
-    V.tensor_tensor(T.t2[:, :], T.t1[:, 0:32], T.t1[:, 32:64], op.add).then_inc(S.u2, 1)
-    V.wait_ge(S.u2, 1)
-    V.tensor_tensor(T.t3[:, :], T.t2[:, 0:16], T.t2[:, 16:32], op.add).then_inc(S.u3, 1)
-    V.wait_ge(S.u3, 1)
-    V.tensor_tensor(T.trep[:, :], T.t3[:, 0:16].indirect(T.mu[:, 0:8]), T.oh[:, :], op.subtract).then_inc(S.u4, 1)
-    V.tensor_scalar(T.rst[:, :], T.kf[:, :], 0.0, None, op.is_gt).then_inc(S.k2, 1)
+    V.tensor_tensor(T.oh[:, :], ext.indirect(T.tu[:, 0:8]), T.kf[:, :], op.is_equal).then_inc(S.o1, 1)
+    V.wait_ge(S.k4, 2)
+    V.tensor_tensor(T.mx[:, :], T.mb[:, :], T.gt[:, :], op.mult).then_inc(S.k6, 1)
+    V.tensor_tensor(T.s2[:, :], T.s1[:, :], T.gt[:, :], op.mult).then_inc(S.k7, 1)
+    V.wait_ge(S.h1, 1)
+    V.tensor_copy(T.x1[:, :], T.px1[:, 0:128]).then_inc(S.w1, 1)
+    V.tensor_scalar(T.sc[:, 1:2], T.pf[:, 0:1], 128.0, T.pf[:, 1:2], op.mult, op.add).then_inc(S.p5, 1)
     V.tensor_scalar(T.kf2[:, :], T.kf[:, :], -7.5, None, op.add).then_inc(S.k2, 1)
+    V.tensor_scalar(T.n16h[:, :], T.cf[:, :], 16.0, BIG, op.mult, op.add).then_inc(S.k2, 1)
+    V.tensor_scalar(T.rst[:, :], T.kf[:, :], 0.0, None, op.is_gt).then_inc(S.k2, 1)
+    V.wait_ge(S.p5, 1)
     V.tensor_scalar(T.jc[:, :], T.ti[:, :], 16.0, T.sc[:, 1:2], op.mult, op.add).then_inc(S.k2, 1)
-    V.wait_ge(S.gi5, 1)
-    V.tensor_scalar(T.n16h[:, :], T.n16[:, :], BIG, None, op.add).then_inc(S.k2, 1)
     V.wait_ge(S.k2, 4)
     V.wait_ge(S.m1, 1)
     V.tensor_tensor_scan(T.vs[:, :], T.rst[:, :], T.pcum[:, 0:128], 0.0, op.mult, op.max).then_inc(S.q2, 1)
@@ -275,95 +296,103 @@ def rank_program(g, core, T, topo):
     V.wait_ge(S.m2, 1)
     V.tensor_copy(T.offs[:, :], T.pidx[:, 0:128]).then_inc(S.of, 1)
 
-    P.wait_ge(S.k1, K1)
+    A.wait_ge(S.h2, 1)
+    A.activation(T.x2[:, :], T.px2[:, 0:128], cp).then_inc(S.w2, 1)
+
+    P.wait_ge(S.k0, 4)
     P.matmul(T.pcum[:, 0:128], T.ones[0:1, :], T.brow[0:1, :], True, False)
     P.matmul(T.pcum[:, 0:128], T.ones[0:1, :], T.neg[0:1, :], False, False)
+    P.wait_ge(S.k1, 3)
     P.wait_ge(S.o1, 1)
-    P.matmul(T.pcum[:, 0:128], T.mac[:, :], T.oh[:, :], False, False)
-    for d in range(1, 8):
-        P.matmul(T.pcum[:, 16 * d:128], T.mb[:, :], T.oh[:, 0:128 - 16 * d], False, False)
-    P.wait_ge(S.u4, 1)
-    P.matmul(T.pcum[:, 0:128], T.ma[:, :], T.trep[:, :], False, True).then_inc(S.m1, 1)
+    P.matmul(T.px1[:, 0:128], T.oh[:, :], T.ma[:, :], True, True).then_inc(S.h1, 1)
+    P.matmul(T.px2[:, 0:128], T.oh[:, :], T.mb[:, :], True, True).then_inc(S.h2, 1)
+    P.wait_ge(S.k5, 1)
+    P.matmul(T.pcum[:, 0:128], T.i4[:, :], T.oh[:, :], False, False)
+    P.wait_ge(S.k6, 1)
+    P.matmul(T.pcum[:, 0:128], T.mx[:, :], T.oh[:, :], False, False)
+    P.wait_ge(S.k4, 2)
+    P.wait_ge(S.w1, 1)
+    P.matmul(T.pcum[:, 0:128], T.x1[:, :], T.s1[:, :], False, False)
+    P.wait_ge(S.k7, 1)
+    P.wait_ge(S.w2, 1)
+    P.matmul(T.pcum[:, 0:128], T.x2[:, :], T.s2[:, :], False, True).then_inc(S.m1, 1)
     for t in range(8):
         c = slice(128 * t, 128 * (t + 1))
         P.wait_ge(S["b%d" % t], 2)
         m = P.matmul(T.pidx[:, 0:128], T.lh[:, c], T.rh[:, c], t == 0, t == 7)
     m.then_inc(S.m2, 1)
 
-    cp = ActivationFunctionType.Copy
-
-    def pack(eng, d, out, sem):
-        src = T.xs[:, 0:1024].indirect(T.offs[:, 16 * d:16 * (d + 1)])
+    def pack(eng, d, out, sem, a=0, b=BLK):
+        src = T.xs[:, 0:1024].indirect(T.offs[:, (BLK * d + a) // 16:(BLK * d + b) // 16])
         if eng == "v":
-            V.tensor_copy(out, src).then_inc(sem, 1)
+            V.tensor_copy(out[:, a:b], src).then_inc(sem, 1)
         else:
-            A.activation(out, src, cp, bias=-0.0).then_inc(sem, 1)
+            A.activation(out[:, a:b], src, cp, bias=-0.0).then_inc(sem, 1)
 
-    for e in (V, A):
-        e.wait_ge(S.of, 1)
-        e.wait_ge(S.xl, 16)
-    for i, (ranks, h) in enumerate(mine):
-        u, v = ranks
-        pack("v", u, T.sb[:, u * BLK:(u + 1) * BLK], S["gv%d" % i])
-        pack("s", v, T.sb[:, v * BLK:(v + 1) * BLK], S["gs%d" % i])
-    pack("v", partner, T.sb[:, partner * BLK:(partner + 1) * BLK], S.gv3)
-    pack("s", rank, T.land[:, rank * BLK:(rank + 1) * BLK], S.gs3)
+    for q in (V, A):
+        q.wait_ge(S.of, 1)
+        q.wait_ge(S.xl, 16)
+    order = [d for call in mine for d, h in call] + [partner]
+    for i, d in enumerate(order):
+        out = T.sb[:, d * BLK:(d + 1) * BLK]
+        if i < 2:
+            pack("v", d, out, S["pk%d" % i], 0, CAPP)
+            pack("s", d, out, S["pk%d" % i], CAPP, BLK)
+        else:
+            pack("vs"[i % 2], d, out, S["pk%d" % i])
+    pack("s", rank, T.land[:, rank * BLK:(rank + 1) * BLK], S.own)
 
-    Y.wait_ge(S.exd, 16)
-    Y.wait_ge(S.meta, meta_total)
-    Y.dma_start(T.xa[:, :], T.exall[:, :, :]).then_inc(S.xal, 16)
     V.memset(T.land[:, N * BLK:LW], 0.0).then_inc(S.kz, 1)
-    V.tensor_scalar(T.sc[:, 2:3], T.pf[:, 3:4], 256.0, None, op.mult).then_inc(S.p5, 1)
-    V.tensor_scalar(T.sc[:, 3:4], T.pf[:, 3:4], 256.0, 256.0, op.mult, op.add).then_inc(S.p5, 1)
-    V.wait_ge(S.p5, 2)
-    V.wait_ge(S.gi6, 1)
-    V.tensor_scalar(T.le[:, :], T.n16[:, :], T.sc[:, 2:3], None, op.is_ge).then_inc(S.k3, 1)
-    V.tensor_scalar(T.nl[:, :], T.n16[:, :], T.sc[:, 3:4], -1.0, op.is_ge, op.mult).then_inc(S.k3, 1)
+    V.tensor_scalar(T.sc[:, 2:3], T.pf[:, 1:2], 16.0, None, op.mult).then_inc(S.p5, 1)
+    V.tensor_scalar(T.sc[:, 3:4], T.pf[:, 1:2], 16.0, 16.0, op.mult, op.add).then_inc(S.p5, 1)
+    V.wait_ge(S.p5, 3)
+    V.wait_ge(S.gi5, 1)
+    V.tensor_scalar(T.le[:, :], T.cf[:, :], T.sc[:, 2:3], None, op.is_ge).then_inc(S.k3, 1)
+    V.tensor_scalar(T.nle[:, :], T.cf[:, :], T.sc[:, 2:3], -1.0, op.is_ge, op.mult).then_inc(S.k3, 1)
+    V.tensor_scalar(T.lt[:, :], T.cf[:, :], T.sc[:, 3:4], None, op.is_ge).then_inc(S.k3, 1)
     V.tensor_scalar(T.rr[:, :], T.kf[:, :], T.pf[:, 2:3], None, op.is_equal).then_inc(S.k3, 1)
     V.tensor_scalar(T.bas[:, :], T.c16[:, :], T.pf[:, 2:3], None, op.add).then_inc(S.k3, 1)
     V.tensor_scalar(T.ip[:, :], T.c16[:, 0:30], T.pf[:, 2:3], None, op.add).then_inc(S.k3, 1)
-    V.wait_ge(S.xal, 16)
+    V.wait_ge(S.meta, meta_total)
     for e in range(EL):
         V.tensor_scalar(T.eqx[:, 64 * e:64 * (e + 1)], T.xa[:, :], float(EL * rank + e), None,
                         op.is_equal).then_inc(S.r1, 1)
-    V.wait_ge(S.r1, 2)
-    for e in range(EL):
-        V.tensor_reduce(T.cnf[:, e:e + 1], T.eqx[:, 64 * e:64 * (e + 1)], AxisListType.X, op.add).then_inc(S.r2, 1)
-    V.wait_ge(S.r2, 2)
-    V.tensor_copy(T.cnb[:, :], T.cnf[:, :]).then_inc(S.r3, 1)
-    P.wait_ge(S.k3, 5)
+    P.wait_ge(S.k3, 6)
     P.matmul(T.prix[:, 0:60], T.rr[0:16, :], T.bas[0:16, :], True, False)
-    P.wait_ge(S.r3, 1)
-    P.matmul(T.pcnt[:, 0:2], T.le[:, :], T.cnb[:, :], True, True)
-    P.matmul(T.pcnt[:, 2:4], T.le[:, :], T.cnb[:, :], True, False)
-    P.matmul(T.pcnt[:, 2:4], T.nl[:, :], T.cnb[:, :], False, True).then_inc(S.m3, 1)
-    V.wait_ge(S.k3, 5)
-    V.wait_ge(S.m3, 1)
-    V.tensor_scalar(T.dl[:, :], T.pcnt[:, 2:4], -1.0, float(BLK), op.mult, op.add).then_inc(S.r4, 1)
-    V.wait_ge(S.r4, 1)
+    P.wait_ge(S.r1, 2)
     for e in range(EL):
-        V.tensor_scalar(T.st[:, 30 * e:30 * (e + 1)], T.ip[:, :], T.pcnt[:, e:e + 1], T.dl[:, e:e + 1], op.is_ge,
+        m = P.matmul(T.pcnt[0:64, 4 + e:5 + e], T.eqx[:, 64 * e:64 * (e + 1)], T.ones[:, 0:1], True, True)
+    m.then_inc(S.r2, 1)
+    V.wait_ge(S.r2, 1)
+    V.tensor_copy(T.cnb[0:64, :], T.pcnt[0:64, 4:6]).then_inc(S.r3, 1)
+    P.wait_ge(S.r3, 1)
+    P.matmul(T.pcnt[:, 0:2], T.le[0:64, :], T.cnb[0:64, :], True, True)
+    P.matmul(T.pcnt[:, 2:4], T.ones[0:1, :], T.c256[0:1, :], True, False)
+    P.matmul(T.pcnt[:, 2:4], T.nle[0:64, :], T.cnb[0:64, :], False, False)
+    P.matmul(T.pcnt[:, 2:4], T.lt[0:64, :], T.cnb[0:64, :], False, True).then_inc(S.m3, 1)
+    V.wait_ge(S.k3, 6)
+    V.wait_ge(S.m3, 1)
+    for e in range(EL):
+        V.tensor_scalar(T.st[:, 30 * e:30 * (e + 1)], T.ip[:, :], T.pcnt[:, e:e + 1], T.pcnt[:, 2 + e:3 + e], op.is_ge,
                         op.mult).then_inc(S.r5, 1)
     P.wait_ge(S.r5, 2)
     P.matmul(T.prix[:, 0:60], T.rr[:, :], T.st[:, :], False, True).then_inc(S.m4, 1)
     V.wait_ge(S.m4, 1)
     V.tensor_copy(T.ro[:, :], T.prix[:, 0:60]).then_inc(S.r6, 1)
 
-    for e in (V, A):
-        e.wait_ge(S.r6, 1)
-        e.wait_ge(S.kz, 1)
-        e.wait_ge(S.gs3, 1)
-        e.wait_ge(S.data, data_total)
+    for q in (V, A):
+        q.wait_ge(S.r6, 1)
+        q.wait_ge(S.kz, 1)
+        q.wait_ge(S.own, 1)
+        q.wait_ge(S.data, data_total)
     hc = HALF // 16
-    V.tensor_copy(T.y0[:, 0:HALF], T.land[:, :].indirect(T.ro[:, 0:hc])).then_inc(S.yva, 1)
-    V.tensor_copy(T.y0[:, HALF:CAP], T.land[:, :].indirect(T.ro[:, hc:30])).then_inc(S.yvb, 1)
-    A.activation(T.y1[:, 0:HALF], T.land[:, :].indirect(T.ro[:, 30:30 + hc]), cp, bias=-0.0).then_inc(S.ysa, 1)
-    A.activation(T.y1[:, HALF:CAP], T.land[:, :].indirect(T.ro[:, 30 + hc:60]), cp, bias=-0.0).then_inc(S.ysb, 1)
-    for sem, src, a, b, o in ((S.yva, T.y0, 0, HALF, 0), (S.ysa, T.y1, 0, HALF, CAP), (S.yvb, T.y0, HALF, CAP, 0)):
-        Y.wait_ge(sem, 1)
-        Y.dma_start(T.y[:, o + a:o + b], src[:, a:b]).then_inc(S.sta, 16)
-    A.wait_ge(S.ysb, 1)
-    A.dma_start(T.y[:, CAP + HALF:2 * CAP], T.y1[:, HALF:CAP]).then_inc(S.stb, 16)
-    Y.wait_ge(S.sta, 48)
-    A.wait_ge(S.stb, 16)
+    for e, y in enumerate((T.y0, T.y1)):
+        V.tensor_copy(y[:, 0:HALF], T.land[:, :].indirect(T.ro[:, 30 * e:30 * e + hc])).then_inc(S["yv%d" % e], 1)
+        A.activation(y[:, HALF:CAP], T.land[:, :].indirect(T.ro[:, 30 * e + hc:30 * (e + 1)]), cp,
+                     bias=-0.0).then_inc(S["ys%d" % e], 1)
+    for e, y in enumerate((T.y0, T.y1)):
+        Y.wait_ge(S["yv%d" % e], 1)
+        Y.wait_ge(S["ys%d" % e], 1)
+        Y.dma_start(T.y[:, CAP * e:CAP * (e + 1)], y[:, :]).then_inc(S.sta, 16)
+    Y.wait_ge(S.sta, 32)
     g.wait_ge(S.loc, loc)

@@ -4,35 +4,38 @@ from concourse.mybir import AluOpType, AxisListType, ActivationFunctionType
 SIM = 128
 N, EL, CAP, CAPP = 8, 2, 480, 128
 BLK = EL * CAPP
-ZC = CAPP + CAP
-LW = N * BLK + ZC
+LW = N * BLK + CAP
 HALF = 256
-BIG = 4096.0
-RND = 201326592.0
+BIG = 256.0
+TV = 7
+WHOLE = [(0, BLK, 0)]
+HALVES = [(0, CAPP, 0), (CAPP, BLK, 1)]
 
 SCRATCH = {
     "xs": ("sbuf", [128, 1024], "float32"),
     "sb": ("sbuf", [128, N * BLK], "float32"),
     "land": ("sbuf", [128, LW], "float32"),
-    "rb": ("sbuf", [128, 2 * BLK], "float32"),
+    "rb": ("sbuf", [128, 3 * BLK], "float32"),
     "y0": ("sbuf", [128, CAP], "float32"),
     "y1": ("sbuf", [128, CAP], "float32"),
     "xa": ("sbuf", [128, N * 8], "int32"),
     "pcol": ("sbuf", [128, 1], "int32"),
     "ti": ("sbuf", [128, 8], "int32"),
     "tu": ("sbuf", [128, 8], "uint16"),
-    "pi": ("sbuf", [128, 3], "int32"),
-    "pf": ("sbuf", [128, 4], "float32"),
+    "pi": ("sbuf", [128, 4], "int32"),
+    "pf": ("sbuf", [128, 8], "float32"),
     "sc": ("sbuf", [128, 4], "float32"),
+    "mk": ("sbuf", [128, 8], "float32"),
     "cf": ("sbuf", [128, 128], "bfloat16"),
     "chf": ("sbuf", [128, 128], "bfloat16"),
     "kf": ("sbuf", [128, 128], "bfloat16"),
-    "kf2": ("sbuf", [128, 128], "bfloat16"),
-    "n16h": ("sbuf", [128, 128], "float16"),
+    "cfb": ("sbuf", [128, 128], "float16"),
+    "cfs": ("sbuf", [128, 128], "float32"),
     "c16": ("sbuf", [128, 60], "float32"),
     "ma": ("sbuf", [128, 128], "bfloat16"),
     "mb": ("sbuf", [128, 128], "bfloat16"),
     "gt": ("sbuf", [128, 128], "bfloat16"),
+    "i4a": ("sbuf", [128, 128], "bfloat16"),
     "i4": ("sbuf", [128, 128], "bfloat16"),
     "mx": ("sbuf", [128, 128], "bfloat16"),
     "s1": ("sbuf", [128, 128], "bfloat16"),
@@ -40,37 +43,40 @@ SCRATCH = {
     "x1": ("sbuf", [128, 128], "bfloat16"),
     "x2": ("sbuf", [128, 128], "bfloat16"),
     "rst": ("sbuf", [128, 128], "float32"),
-    "brow": ("sbuf", [128, 128], "bfloat16"),
-    "neg": ("sbuf", [128, 128], "bfloat16"),
     "ones": ("sbuf", [128, 128], "bfloat16"),
-    "c256": ("sbuf", [128, 2], "bfloat16"),
+    "dr": ("sbuf", [128, 256], "bfloat16"),
     "jc": ("sbuf", [128, 8], "float32"),
     "oh": ("sbuf", [128, 128], "bfloat16"),
+    "ohj": ("sbuf", [128, 128], "float16"),
     "vs": ("sbuf", [128, 128], "float32"),
-    "v16": ("sbuf", [128, 8], "float32"),
     "lh": ("sbuf", [128, 1024], "float16"),
-    "rh": ("sbuf", [128, 1024], "float16"),
+    "za": ("sbuf", [128, 1024], "float32"),
+    "ls": ("sbuf", [128, 1024], "bfloat16"),
+    "gf": ("sbuf", [128, 16], "float16"),
+    "rsp": ("sbuf", [128, 1024], "bfloat16"),
     "offs": ("sbuf", [128, 128], "uint16"),
     "le": ("sbuf", [128, 128], "bfloat16"),
     "nle": ("sbuf", [128, 128], "bfloat16"),
     "lt": ("sbuf", [128, 128], "bfloat16"),
-    "rr": ("sbuf", [128, 128], "float16"),
-    "bas": ("sbuf", [128, 60], "float16"),
+    "rr": ("sbuf", [128, 128], "float32"),
+    "bas": ("sbuf", [128, 60], "float32"),
     "ip": ("sbuf", [128, 30], "float32"),
     "eqx": ("sbuf", [128, 128], "bfloat16"),
     "cnb": ("sbuf", [128, 2], "bfloat16"),
-    "st": ("sbuf", [128, 60], "float16"),
+    "st": ("sbuf", [128, 60], "float32"),
     "ro": ("sbuf", [128, 60], "uint16"),
     "px1": ("psum", [128, 512], "float32"),
     "px2": ("psum", [128, 512], "float32"),
     "pcum": ("psum", [128, 512], "float32"),
+    "pg": ("psum", [128, 512], "float32"),
     "pidx": ("psum", [128, 512], "float32"),
     "pcnt": ("psum", [128, 512], "float32"),
     "prix": ("psum", [128, 512], "float32"),
 }
-SEMAPHORES = (["meta", "data", "rb0", "rb1", "loc", "exs", "xl", "sta"]
-              + ["gi%d" % i for i in range(6)] + ["p1", "p2", "p5", "k0", "k1", "k2", "k3", "k4", "k5", "k6", "k7", "kz"]
-              + ["o1", "h1", "h2", "w1", "w2", "m1", "m2", "m3", "m4", "q2", "q4", "of"]
+SEMAPHORES = (["meta", "data0", "data1", "rb0", "rb1", "rb2", "loc", "exs", "xl", "sta"]
+              + ["gi%d" % i for i in range(6)] + ["p1", "p2", "p5", "p6", "k0", "k1", "k2", "k3", "k4", "k5", "k6", "k7", "k8"]
+              + ["k9", "kc", "kd", "kq", "ks", "kr", "kz", "oj", "z6"]
+              + ["o1", "h1", "h2", "w1", "w2", "m1", "m2", "m3", "m4", "m5", "q2", "gq", "of"]
               + ["b%d" % i for i in range(8)] + ["pk%d" % i for i in range(7)] + ["own"]
               + ["r1", "r2", "r3", "r5", "r6", "yv0", "yv1", "ys0", "ys1"])
 
@@ -109,19 +115,20 @@ def routes(cores, topo):
         if mate[cs] in chips and far:
             m = on[mate[cs]]
             (a0, a1), (b0, b1) = [on[x] for x in far]
-            ra, rb = [relays(mate[x], die, on[x][:1])[0] for x in far]
+            away = [(d, relays(mate[topo.chip(cores[d])], die, [d])[0]) for d in (a0, b0, a1)]
             h0, h1 = relays(cs, die, m)
             if barred:
-                away = [(a0, ra), (b0, rb), (a1, relays(mate[far[0]], die, [a1])[0])]
                 here = [(b1, h1), (m[0], h0), (m[1], h0)]
             else:
-                away = [(a0, ra), (b0, rb), (b1, None), (a1, None)]
-                here = [(m[0], h0), (m[1], h1)]
+                here = [(m[0], h0), (m[1], h1), (b1, h1)]
         else:
             hand = (barred or [x for x in others if topo.same_plane(cs, x)])[-1]
             here = list(zip(on[hand], relays(cs, die, on[hand])))
-            away = [(d, None) for x in others if x != hand for d in on[x]]
-        plan.append([[away[0]], [here[0]], [away[1], here[1]], away[2:] + here[2:]])
+            rest = [d for x in others if x != hand for d in on[x]]
+            more = [d for d in rest if topo.same_plane(cs, topo.chip(cores[d]))][-1]
+            here.append((more, relays(cs, die, [more])[0]))
+            away = [(d, None) for d in rest if d != more]
+        plan.append([[away[0]], [here[0]], [away[1], here[1]], [here[2]], [away[2]]])
     return plan
 
 
@@ -131,6 +138,35 @@ def jobs_of(plan, core):
         if mine:
             return r, mine
     return None, []
+
+
+def pieces(ds, i):
+    return HALVES if i == len(ds) - 1 else WHOLE
+
+
+def cuts(calls, call):
+    return HALVES if call is calls[-1] and all(h is None for d, h in call) else WHOLE
+
+
+def layout(plan, d):
+    halved = []
+    for r, calls in enumerate(plan):
+        for call in calls:
+            for b, h in call:
+                ds = jobs_of(plan, h)[1]
+                if b == d and (cuts(calls, call) if h is None else pieces(ds, ds.index(d))) is HALVES:
+                    halved.append(r)
+    w0 = CAPP * len(halved)
+    z0 = w0 + BLK * (N - len(halved))
+    at, w = {}, w0
+    for r in range(N):
+        if r in halved:
+            i = halved.index(r)
+            at[r] = (CAPP * i, z0 + CAP + CAPP * i)
+        else:
+            at[r] = (w, w + CAPP)
+            w += BLK
+    return at, w0, z0
 
 
 def masks(core, topo):
@@ -168,14 +204,18 @@ def relay_program(g, core, T, topo, plan, r, ds):
     src = T.cores[r]
     g.wait_ge(T.sem.meta, len(engines(src, [core], topo)[0]))
     g.remote_dma_fused([cast(T, topo, r, [T.cores[d] for d in ds], off)], local_sem=T.sem.loc)
+    loc = len(off)
     for i, d in enumerate(ds):
         call = [c for c in plan[r] if (d, core) in c][0]
         eng = engines(src, [T.cores[b] if h is None else h for b, h in call], topo)[call.index((d, core))]
         g.wait_ge(T.sem["rb%d" % i], len(eng))
         rid, pid, _ = topo.addr(T.cores[d])
-        g.remote_dma(T.land[:, r * BLK:(r + 1) * BLK], T.rb[:, i * BLK:(i + 1) * BLK], T.sem.data, T.sem.loc, pid, rid,
-                     join(off))
-    g.wait_ge(T.sem.loc, (1 + len(ds)) * len(off))
+        for a, b, s in pieces(ds, i):
+            lo = layout(plan, d)[0][r][s]
+            g.remote_dma(T.land[:, lo:lo + b - a], T.rb[:, i * BLK + a:i * BLK + b], T.sem["data%d" % s],
+                         T.sem.loc, pid, rid, join(off))
+            loc += len(off)
+    g.wait_ge(T.sem.loc, loc)
 
 
 def rank_program(g, core, T, topo):
@@ -194,7 +234,7 @@ def rank_program(g, core, T, topo):
     partner = [i for i, c in enumerate(cores) if topo.chip(c) == topo.chip(core) and i != rank][0]
     off, near = masks(core, topo)
     meta_total = len(near)
-    data_total = len(near)
+    data_total = [len(near), 0]
     for r in range(N):
         for call in plan[r]:
             to = [cores[d] if h is None else h for d, h in call]
@@ -202,7 +242,13 @@ def rank_program(g, core, T, topo):
                 if d == rank:
                     full = masks(cores[r] if h is None else h, topo)[0]
                     meta_total += len(full)
-                    data_total += len(e) if h is None else len(full)
+                    ds = jobs_of(plan, h)[1]
+                    for a, b, s in cuts(plan[r], call) if h is None else pieces(ds, ds.index(d)):
+                        data_total[s] += len(e) if h is None else len(full)
+    at, w0, z0 = layout(plan, rank)
+    first = [0, w0]
+    end = [z0 + CAP, LW]
+    place = [[at[r][e] - first[e] for r in range(N)] + [z0 - first[e]] for e in range(EL)]
 
     ext = T.xa[:, 8 * rank:8 * rank + 8]
     Y.dma_start(ext, T.ex[:, :]).then_inc(S.exs, 16)
@@ -220,107 +266,150 @@ def rank_program(g, core, T, topo):
     g.wait_ge(S.exs, 16)
     g.remote_dma_fused([cast(T, topo, rank, out_, off), cast(T, topo, rank, in_, near)], local_sem=S.loc)
     loc = len(off) + len(near)
-    g.iota(T.c16[:, :], [[128, 2], [16, 30]], 0, 0, **imp).then_inc(S.gi5, 1)
+    g.iota(T.c16[:, :], [[place[1][0] - place[0][0], EL], [16, CAP // 16]], place[0][0], 0, **imp).then_inc(S.gi5, 1)
     n = 0
     for call in mine:
-        tr = []
         to = [cores[d] if h is None else h for d, h in call]
-        for (d, h), c, eng in zip(call, to, engines(core, to, topo)):
-            g.wait_ge(S["pk%d" % n], 2 if n < 2 else 1)
-            n += 1
-            if h is None:
-                sem, dst = S.data, T.land[:, rank * BLK:(rank + 1) * BLK]
-            else:
-                k = jobs_of(plan, h)[1].index(d)
-                sem, dst = S["rb%d" % k], T.rb[:, k * BLK:(k + 1) * BLK]
-            tr.append(RemoteDMATransfer(dst_ids=[ident(topo, c)], dma_engine_mask=join(eng), remote_sem=sem,
-                                        srcs=[T.sb[:, d * BLK:(d + 1) * BLK]], dsts=[dst]))
-            loc += len(eng)
-        g.remote_dma_fused(tr, local_sem=S.loc)
+        for a, b, s in cuts(mine, call):
+            tr = []
+            for (d, h), c, eng in zip(call, to, engines(core, to, topo)):
+                if a == 0:
+                    g.wait_ge(S["pk%d" % n], 2 if n < 2 else 1)
+                    n += 1
+                if h is None:
+                    lo = layout(plan, d)[0][rank][s]
+                    sem, dst = S["data%d" % s], T.land[:, lo:lo + b - a]
+                else:
+                    k = jobs_of(plan, h)[1].index(d)
+                    sem, dst = S["rb%d" % k], T.rb[:, k * BLK:(k + 1) * BLK]
+                tr.append(RemoteDMATransfer(dst_ids=[ident(topo, c)], dma_engine_mask=join(eng), remote_sem=sem,
+                                            srcs=[T.sb[:, d * BLK + a:d * BLK + b]], dsts=[dst]))
+                loc += len(eng)
+            g.remote_dma_fused(tr, local_sem=S.loc)
     g.wait_ge(S.pk6, 1)
     rid, pid, _ = topo.addr(cores[partner])
-    g.remote_dma(T.land[:, rank * BLK:(rank + 1) * BLK], T.sb[:, partner * BLK:(partner + 1) * BLK], S.data, S.loc,
-                 pid, rid, join(near))
+    lo = layout(plan, partner)[0][rank][0]
+    g.remote_dma(T.land[:, lo:lo + BLK], T.sb[:, partner * BLK:(partner + 1) * BLK], S.data0, S.loc, pid, rid, join(near))
     loc += len(near)
 
-    cp = ActivationFunctionType.Copy
+    fn = ActivationFunctionType
+    cp = fn.Copy
+
+    def spread(eng, i):
+        out, col = T.rsp[:, 128 * i:128 * (i + 1)], T.mk[:, i:i + 1]
+        if eng == "v":
+            V.tensor_scalar(out, T.s1[:, :], col, None, op.mult).then_inc(S.kr, 1)
+        else:
+            A.activation(out, T.s1[:, :], cp, scale=col).then_inc(S.kr, 1)
+
     A.wait_ge(S.gi1, 1)
     A.activation(T.ones[:, :], T.kf[:, :], cp, bias=1.0, scale=0.0).then_inc(S.k0, 1)
-    A.activation(T.brow[:, :], T.kf[:, :], cp, scale=128.0).then_inc(S.k0, 1)
-    A.activation(T.neg[:, :], T.kf[:, :], cp, bias=-7.5, scale=0.0).then_inc(S.k0, 1)
-    A.activation(T.c256[:, :], T.kf[:, 0:2], cp, bias=float(BLK), scale=0.0).then_inc(S.k0, 1)
+    A.activation(T.rst[:, :], T.kf[:, :], fn.Sign).then_inc(S.kc, 1)
+    A.wait_ge(S.k4, 1)
+    A.wait_ge(S.k9, 1)
+    for i in (0, 1, 2):
+        spread("s", i)
+    A.wait_ge(S.gi4, 1)
+    A.wait_ge(S.p2, 2)
+    A.activation(T.i4a[:, :], T.cf[:, :], fn.Abs, bias=T.pf[:, 4:5], scale=-1.0).then_inc(S.k5, 1)
+    A.wait_ge(S.k5, 1)
+    A.activation(T.i4[:, :], T.i4a[:, :], fn.Relu, bias=BIG, scale=-BIG).then_inc(S.kd, 1)
 
     V.wait_ge(S.gi0, 1)
-    for i, (o, c) in enumerate([(op.bitwise_and, 7), (op.logical_shift_right, 3), (op.bitwise_and, 15)]):
+    for i, (o, c) in enumerate([(op.bitwise_and, 7), (op.logical_shift_right, 3), (op.bitwise_and, 15),
+                                (op.logical_shift_right, 4)]):
         V.tensor_scalar(T.pi[:, i:i + 1], T.pcol[:, :], c, None, o).then_inc(S.p1, 1)
-    V.tensor_copy(T.pf[:, 3:4], T.pcol[:, :]).then_inc(S.p2, 1)
-    V.wait_ge(S.p1, 3)
-    V.tensor_copy(T.pf[:, 0:3], T.pi[:, :]).then_inc(S.p2, 1)
-    V.wait_ge(S.gi2, 1)
-    V.tensor_copy(T.tu[:, :], T.ti[:, :]).then_inc(S.k1, 1)
-    V.wait_ge(S.p2, 2)
+    V.tensor_copy(T.pf[:, 4:5], T.pcol[:, :]).then_inc(S.p2, 1)
+    V.wait_ge(S.p1, 4)
+    V.tensor_copy(T.pf[:, 0:4], T.pi[:, :]).then_inc(S.p2, 1)
     V.wait_ge(S.gi1, 1)
+    V.wait_ge(S.p2, 2)
+    V.tensor_scalar(T.sc[:, 1:2], T.pf[:, 0:1], 128.0, T.pf[:, 1:2], op.mult, op.add).then_inc(S.p5, 1)
     V.tensor_scalar(T.s1[:, :], T.kf[:, :], T.pf[:, 2:3], None, op.is_equal).then_inc(S.k4, 1)
+    V.wait_ge(S.gi2, 1)
+    V.tensor_scalar(T.mk[:, :], T.ti[:, :], T.pf[:, 3:4], None, op.is_equal).then_inc(S.k9, 1)
+    V.tensor_copy(T.tu[:, :], T.ti[:, :]).then_inc(S.k1, 1)
+    V.wait_ge(S.p5, 1)
+    V.tensor_scalar(T.jc[:, :], T.ti[:, :], 16.0, T.sc[:, 1:2], op.mult, op.add).then_inc(S.k2, 1)
     V.wait_ge(S.gi3, 1)
     V.tensor_scalar(T.ma[:, :], T.chf[:, :], T.pf[:, 0:1], None, op.is_gt).then_inc(S.k1, 1)
     V.tensor_scalar(T.mb[:, :], T.chf[:, :], T.pf[:, 0:1], None, op.is_equal).then_inc(S.k1, 1)
-    V.wait_ge(S.gi4, 1)
-    V.tensor_scalar(T.gt[:, :], T.cf[:, :], T.pf[:, 3:4], None, op.is_gt).then_inc(S.k4, 1)
-    V.tensor_scalar(T.i4[:, :], T.cf[:, :], T.pf[:, 3:4], BIG, op.is_equal, op.mult).then_inc(S.k5, 1)
     V.wait_ge(S.k1, 3)
     V.wait_ge(S.exs, 16)
     V.tensor_tensor(T.oh[:, :], ext.indirect(T.tu[:, 0:8]), T.kf[:, :], op.is_equal).then_inc(S.o1, 1)
-    V.wait_ge(S.k4, 2)
-    V.tensor_tensor(T.mx[:, :], T.mb[:, :], T.gt[:, :], op.mult).then_inc(S.k6, 1)
+    V.wait_ge(S.gi4, 1)
+    V.tensor_scalar(T.gt[:, :], T.cf[:, :], T.pf[:, 4:5], None, op.is_gt).then_inc(S.k8, 1)
+    V.wait_ge(S.k4, 1)
+    V.wait_ge(S.k8, 1)
     V.tensor_tensor(T.s2[:, :], T.s1[:, :], T.gt[:, :], op.mult).then_inc(S.k7, 1)
-    V.wait_ge(S.h1, 1)
-    V.tensor_copy(T.x1[:, :], T.px1[:, 0:128]).then_inc(S.w1, 1)
-    V.tensor_scalar(T.sc[:, 1:2], T.pf[:, 0:1], 128.0, T.pf[:, 1:2], op.mult, op.add).then_inc(S.p5, 1)
-    V.tensor_scalar(T.kf2[:, :], T.kf[:, :], -7.5, None, op.add).then_inc(S.k2, 1)
-    V.tensor_scalar(T.n16h[:, :], T.cf[:, :], 16.0, BIG, op.mult, op.add).then_inc(S.k2, 1)
-    V.tensor_scalar(T.rst[:, :], T.kf[:, :], 0.0, None, op.is_gt).then_inc(S.k2, 1)
-    V.wait_ge(S.p5, 1)
-    V.tensor_scalar(T.jc[:, :], T.ti[:, :], 16.0, T.sc[:, 1:2], op.mult, op.add).then_inc(S.k2, 1)
-    V.wait_ge(S.k2, 4)
+    V.tensor_tensor(T.mx[:, :], T.mb[:, :], T.gt[:, :], op.mult).then_inc(S.k6, 1)
+    V.tensor_scalar(T.cfb[:, :], T.cf[:, :], BIG, None, op.add).then_inc(S.k2, 1)
+    V.wait_ge(S.k9, 1)
+    for i in (3, 4):
+        spread("v", i)
+    V.wait_ge(S.k2, 2)
+    V.wait_ge(S.kc, 1)
     V.wait_ge(S.m1, 1)
     V.tensor_tensor_scan(T.vs[:, :], T.rst[:, :], T.pcum[:, 0:128], 0.0, op.mult, op.max).then_inc(S.q2, 1)
     V.wait_ge(S.q2, 1)
-    V.tensor_scalar(T.v16[:, :], T.vs[:, 15::16], RND, RND, op.add, op.subtract).then_inc(S.q4, 1)
-    V.wait_ge(S.q4, 1)
-    for t in range(8):
-        c = slice(128 * t, 128 * (t + 1))
-        V.tensor_scalar(T.lh[:, c], T.kf2[:, :], T.v16[:, t:t + 1], T.vs[:, 16 * t + 15:16 * t + 16], op.add,
-                        op.is_equal).then_inc(S["b%d" % t], 1)
-        V.tensor_scalar(T.rh[:, c], T.n16h[:, :], T.v16[:, t:t + 1], T.jc[:, t:t + 1], op.is_equal,
-                        op.mult).then_inc(S["b%d" % t], 1)
+    for t in range(TV):
+        V.tensor_scalar(T.lh[:, 128 * t:128 * (t + 1)], T.cfb[:, :], T.vs[:, 16 * t + 15:16 * t + 16], T.jc[:, t:t + 1],
+                        op.is_equal, op.mult).then_inc(S["b%d" % t], 1)
+        if t == 0:
+            V.wait_ge(S.o1, 1)
+            for u in range(TV, 8):
+                V.tensor_scalar(T.ohj[:, 16 * u:16 * (u + 1)], T.oh[:, 16 * u:16 * (u + 1)], T.jc[:, u:u + 1], None,
+                                op.mult).then_inc(S.oj, 1)
     V.wait_ge(S.m2, 1)
+    V.tensor_copy(T.gf[:, :], T.pg[:, 0:16]).then_inc(S.gq, 1)
+    V.wait_ge(S.m5, 1)
     V.tensor_copy(T.offs[:, :], T.pidx[:, 0:128]).then_inc(S.of, 1)
 
+    A.wait_ge(S.h1, 1)
+    A.activation(T.x1[:, :], T.px1[:, 0:128], cp).then_inc(S.w1, 1)
     A.wait_ge(S.h2, 1)
     A.activation(T.x2[:, :], T.px2[:, 0:128], cp).then_inc(S.w2, 1)
+    A.activation(T.cfs[:, :], T.cf[:, :], cp, bias=BIG).then_inc(S.ks, 1)
+    spread("s", 5)
+    A.wait_ge(S.ks, 1)
+    A.wait_ge(S.q2, 1)
+    for t in range(TV, 8):
+        A.activation(T.za[:, 128 * t:128 * (t + 1)], T.cfs[:, :], fn.Abs, bias=T.vs[:, 16 * t + 15:16 * t + 16],
+                     scale=-1.0).then_inc(S.z6, 1)
+    A.wait_ge(S.z6, 8 - TV)
+    for t in range(TV, 8):
+        A.activation(T.ls[:, 128 * t:128 * (t + 1)], T.za[:, 128 * t:128 * (t + 1)], fn.Relu, bias=1.0,
+                     scale=-1.0).then_inc(S["b%d" % t], 1)
+    for i in (6, 7):
+        spread("s", i)
 
-    P.wait_ge(S.k0, 4)
-    P.matmul(T.pcum[:, 0:128], T.ones[0:1, :], T.brow[0:1, :], True, False)
-    P.matmul(T.pcum[:, 0:128], T.ones[0:1, :], T.neg[0:1, :], False, False)
     P.wait_ge(S.k1, 3)
     P.wait_ge(S.o1, 1)
     P.matmul(T.px1[:, 0:128], T.oh[:, :], T.ma[:, :], True, True).then_inc(S.h1, 1)
     P.matmul(T.px2[:, 0:128], T.oh[:, :], T.mb[:, :], True, True).then_inc(S.h2, 1)
-    P.wait_ge(S.k5, 1)
-    P.matmul(T.pcum[:, 0:128], T.i4[:, :], T.oh[:, :], False, False)
-    P.wait_ge(S.k6, 1)
-    P.matmul(T.pcum[:, 0:128], T.mx[:, :], T.oh[:, :], False, False)
-    P.wait_ge(S.k4, 2)
+    P.wait_ge(S.kd, 1)
+    P.matmul(T.pcum[:, 0:128], T.i4[:, :], T.oh[:, :], True, False)
+    P.wait_ge(S.k4, 1)
     P.wait_ge(S.w1, 1)
     P.matmul(T.pcum[:, 0:128], T.x1[:, :], T.s1[:, :], False, False)
     P.wait_ge(S.k7, 1)
     P.wait_ge(S.w2, 1)
-    P.matmul(T.pcum[:, 0:128], T.x2[:, :], T.s2[:, :], False, True).then_inc(S.m1, 1)
-    for t in range(8):
-        c = slice(128 * t, 128 * (t + 1))
-        P.wait_ge(S["b%d" % t], 2)
-        m = P.matmul(T.pidx[:, 0:128], T.lh[:, c], T.rh[:, c], t == 0, t == 7)
+    P.matmul(T.pcum[:, 0:128], T.x2[:, :], T.s2[:, :], False, False)
+    P.wait_ge(S.k6, 1)
+    P.matmul(T.pcum[:, 0:128], T.mx[:, :], T.oh[:, :], False, True).then_inc(S.m1, 1)
+    turn = list(range(4)) + list(range(TV, 8)) + list(range(4, TV))
+    for t in turn:
+        P.wait_ge(S["b%d" % t], 1)
+        if t == TV:
+            P.wait_ge(S.oj, 8 - TV)
+        lhs, rhs = (T.lh, T.oh) if t < TV else (T.ls, T.ohj)
+        m = P.matmul(T.pg[:, 0:16], lhs[:, 128 * t:128 * (t + 1)], rhs[:, 16 * t:16 * (t + 1)], t == turn[0], t == turn[-1])
     m.then_inc(S.m2, 1)
+    P.wait_ge(S.kr, 8)
+    P.wait_ge(S.gq, 1)
+    for i in range(8):
+        m = P.matmul(T.pidx[:, i:128:8], T.rsp[:, 128 * i:128 * (i + 1)], T.gf[:, :], True, True)
+    m.then_inc(S.m5, 1)
 
     def pack(eng, d, out, sem, a=0, b=BLK):
         src = T.xs[:, 0:1024].indirect(T.offs[:, (BLK * d + a) // 16:(BLK * d + b) // 16])
@@ -340,25 +429,39 @@ def rank_program(g, core, T, topo):
             pack("s", d, out, S["pk%d" % i], CAPP, BLK)
         else:
             pack("vs"[i % 2], d, out, S["pk%d" % i])
-    pack("s", rank, T.land[:, rank * BLK:(rank + 1) * BLK], S.own)
+    pack("s", rank, T.land[:, at[rank][0]:at[rank][0] + BLK], S.own)
 
-    V.memset(T.land[:, N * BLK:LW], 0.0).then_inc(S.kz, 1)
-    V.tensor_scalar(T.sc[:, 2:3], T.pf[:, 1:2], 16.0, None, op.mult).then_inc(S.p5, 1)
-    V.tensor_scalar(T.sc[:, 3:4], T.pf[:, 1:2], 16.0, 16.0, op.mult, op.add).then_inc(S.p5, 1)
-    V.wait_ge(S.p5, 3)
+    nq = 0
+    for e in range(EL):
+        step = [place[e][r + 1] - place[e][r] for r in range(N)]
+        r = 0
+        while r < N:
+            q = r
+            while q < N and step[q] == step[r]:
+                q += 1
+            A.activation(T.dr[0:1, 128 * e + 16 * r:128 * e + 16 * q], T.kf[0:1, 16 * r:16 * q], cp, bias=float(step[r]),
+                         scale=0.0).then_inc(S.kq, 1)
+            nq += 1
+            r = q
+    V.memset(T.land[:, z0:z0 + CAP], 0.0).then_inc(S.kz, 1)
+    V.tensor_scalar(T.sc[:, 2:3], T.pf[:, 1:2], 16.0, None, op.mult).then_inc(S.p6, 1)
+    V.tensor_scalar(T.sc[:, 3:4], T.pf[:, 1:2], 16.0, 16.0, op.mult, op.add).then_inc(S.p6, 1)
+    V.wait_ge(S.p6, 2)
     V.wait_ge(S.gi5, 1)
     V.tensor_scalar(T.le[:, :], T.cf[:, :], T.sc[:, 2:3], None, op.is_ge).then_inc(S.k3, 1)
     V.tensor_scalar(T.nle[:, :], T.cf[:, :], T.sc[:, 2:3], -1.0, op.is_ge, op.mult).then_inc(S.k3, 1)
     V.tensor_scalar(T.lt[:, :], T.cf[:, :], T.sc[:, 3:4], None, op.is_ge).then_inc(S.k3, 1)
     V.tensor_scalar(T.rr[:, :], T.kf[:, :], T.pf[:, 2:3], None, op.is_equal).then_inc(S.k3, 1)
     V.tensor_scalar(T.bas[:, :], T.c16[:, :], T.pf[:, 2:3], None, op.add).then_inc(S.k3, 1)
-    V.tensor_scalar(T.ip[:, :], T.c16[:, 0:30], T.pf[:, 2:3], None, op.add).then_inc(S.k3, 1)
+    V.tensor_scalar(T.ip[:, :], T.c16[:, 0:30], T.pf[:, 2:3], float(place[0][0]), op.add,
+                    op.subtract).then_inc(S.k3, 1)
     V.wait_ge(S.meta, meta_total)
     for e in range(EL):
         V.tensor_scalar(T.eqx[:, 64 * e:64 * (e + 1)], T.xa[:, :], float(EL * rank + e), None,
                         op.is_equal).then_inc(S.r1, 1)
     P.wait_ge(S.k3, 6)
     P.matmul(T.prix[:, 0:60], T.rr[0:16, :], T.bas[0:16, :], True, False)
+    P.wait_ge(S.k0, 1)
     P.wait_ge(S.r1, 2)
     for e in range(EL):
         m = P.matmul(T.pcnt[0:64, 4 + e:5 + e], T.eqx[:, 64 * e:64 * (e + 1)], T.ones[:, 0:1], True, True)
@@ -367,9 +470,12 @@ def rank_program(g, core, T, topo):
     V.tensor_copy(T.cnb[0:64, :], T.pcnt[0:64, 4:6]).then_inc(S.r3, 1)
     P.wait_ge(S.r3, 1)
     P.matmul(T.pcnt[:, 0:2], T.le[0:64, :], T.cnb[0:64, :], True, True)
-    P.matmul(T.pcnt[:, 2:4], T.ones[0:1, :], T.c256[0:1, :], True, False)
-    P.matmul(T.pcnt[:, 2:4], T.nle[0:64, :], T.cnb[0:64, :], False, False)
-    P.matmul(T.pcnt[:, 2:4], T.lt[0:64, :], T.cnb[0:64, :], False, True).then_inc(S.m3, 1)
+    P.wait_ge(S.kq, nq)
+    for e in range(EL):
+        P.matmul(T.pcnt[:, 2 + e:3 + e], T.dr[0:1, 128 * e:128 * (e + 1)], T.ones[0:1, 0:1], True, False)
+        P.matmul(T.pcnt[:, 2 + e:3 + e], T.nle[0:64, :], T.cnb[0:64, e:e + 1], False, False)
+        m = P.matmul(T.pcnt[:, 2 + e:3 + e], T.lt[0:64, :], T.cnb[0:64, e:e + 1], False, True)
+    m.then_inc(S.m3, 1)
     V.wait_ge(S.k3, 6)
     V.wait_ge(S.m3, 1)
     for e in range(EL):
@@ -384,11 +490,14 @@ def rank_program(g, core, T, topo):
         q.wait_ge(S.r6, 1)
         q.wait_ge(S.kz, 1)
         q.wait_ge(S.own, 1)
-        q.wait_ge(S.data, data_total)
     hc = HALF // 16
     for e, y in enumerate((T.y0, T.y1)):
-        V.tensor_copy(y[:, 0:HALF], T.land[:, :].indirect(T.ro[:, 30 * e:30 * e + hc])).then_inc(S["yv%d" % e], 1)
-        A.activation(y[:, HALF:CAP], T.land[:, :].indirect(T.ro[:, 30 * e + hc:30 * (e + 1)]), cp,
+        if data_total[e]:
+            V.wait_ge(S["data%d" % e], data_total[e])
+            A.wait_ge(S["data%d" % e], data_total[e])
+        win = T.land[:, first[e]:end[e]]
+        V.tensor_copy(y[:, 0:HALF], win.indirect(T.ro[:, 30 * e:30 * e + hc])).then_inc(S["yv%d" % e], 1)
+        A.activation(y[:, HALF:CAP], win.indirect(T.ro[:, 30 * e + hc:30 * (e + 1)]), cp,
                      bias=-0.0).then_inc(S["ys%d" % e], 1)
     for e, y in enumerate((T.y0, T.y1)):
         Y.wait_ge(S["yv%d" % e], 1)

from concourse.bass import DstId, RemoteDMATransfer
from concourse.mybir import AluOpType, AxisListType, ActivationFunctionType

SIM = 128
N, EL, CAP, CAPP = 8, 2, 480, 128
BLK = EL * CAPP
LW = N * BLK + CAP
HALF = 256
BIG = 256.0
TV = 7
WHOLE = [(0, BLK, 0)]
HALVES = [(0, CAPP, 0), (CAPP, BLK, 1)]

SCRATCH = {
    "xs": ("sbuf", [128, 1024], "float32"),
    "sb": ("sbuf", [128, N * BLK], "float32"),
    "land": ("sbuf", [128, LW], "float32"),
    "rb": ("sbuf", [128, 3 * BLK], "float32"),
    "y0": ("sbuf", [128, CAP], "float32"),
    "y1": ("sbuf", [128, CAP], "float32"),
    "xa": ("sbuf", [128, N * 8], "int32"),
    "pcol": ("sbuf", [128, 1], "int32"),
    "ti": ("sbuf", [128, 8], "int32"),
    "tu": ("sbuf", [128, 8], "uint16"),
    "pi": ("sbuf", [128, 4], "int32"),
    "pf": ("sbuf", [128, 8], "float32"),
    "sc": ("sbuf", [128, 4], "float32"),
    "mk": ("sbuf", [128, 8], "float32"),
    "cf": ("sbuf", [128, 128], "bfloat16"),
    "chf": ("sbuf", [128, 128], "bfloat16"),
    "kf": ("sbuf", [128, 128], "bfloat16"),
    "cfb": ("sbuf", [128, 128], "float16"),
    "cfs": ("sbuf", [128, 128], "float32"),
    "c16": ("sbuf", [128, 60], "float32"),
    "ma": ("sbuf", [128, 128], "bfloat16"),
    "mb": ("sbuf", [128, 128], "bfloat16"),
    "gt": ("sbuf", [128, 128], "bfloat16"),
    "i4a": ("sbuf", [128, 128], "bfloat16"),
    "i4": ("sbuf", [128, 128], "bfloat16"),
    "mx": ("sbuf", [128, 128], "bfloat16"),
    "s1": ("sbuf", [128, 128], "bfloat16"),
    "s2": ("sbuf", [128, 128], "bfloat16"),
    "x1": ("sbuf", [128, 128], "bfloat16"),
    "x2": ("sbuf", [128, 128], "bfloat16"),
    "rst": ("sbuf", [128, 128], "float32"),
    "ones": ("sbuf", [128, 128], "bfloat16"),
    "dr": ("sbuf", [128, 256], "bfloat16"),
    "jc": ("sbuf", [128, 8], "float32"),
    "oh": ("sbuf", [128, 128], "bfloat16"),
    "ohj": ("sbuf", [128, 128], "float16"),
    "vs": ("sbuf", [128, 128], "float32"),
    "lh": ("sbuf", [128, 1024], "float16"),
    "za": ("sbuf", [128, 1024], "float32"),
    "ls": ("sbuf", [128, 1024], "bfloat16"),
    "gf": ("sbuf", [128, 16], "float16"),
    "rsp": ("sbuf", [128, 1024], "bfloat16"),
    "offs": ("sbuf", [128, 128], "uint16"),
    "le": ("sbuf", [128, 128], "bfloat16"),
    "nle": ("sbuf", [128, 128], "bfloat16"),
    "lt": ("sbuf", [128, 128], "bfloat16"),
    "rr": ("sbuf", [128, 128], "float32"),
    "bas": ("sbuf", [128, 60], "float32"),
    "ip": ("sbuf", [128, 30], "float32"),
    "eqx": ("sbuf", [128, 128], "bfloat16"),
    "cnb": ("sbuf", [128, 2], "bfloat16"),
    "st": ("sbuf", [128, 60], "float32"),
    "ro": ("sbuf", [128, 60], "uint16"),
    "px1": ("psum", [128, 512], "float32"),
    "px2": ("psum", [128, 512], "float32"),
    "pcum": ("psum", [128, 512], "float32"),
    "pg": ("psum", [128, 512], "float32"),
    "pidx": ("psum", [128, 512], "float32"),
    "pcnt": ("psum", [128, 512], "float32"),
    "prix": ("psum", [128, 512], "float32"),
}
SEMAPHORES = (["meta", "data0", "data1", "rb0", "rb1", "rb2", "loc", "exs", "xl", "sta"]
              + ["gi%d" % i for i in range(6)] + ["p1", "p2", "p5", "p6", "k0", "k1", "k2", "k3", "k4", "k5", "k6", "k7", "k8"]
              + ["k9", "kc", "kd", "kq", "ks", "kr", "kz", "oj", "z6"]
              + ["o1", "h1", "h2", "w1", "w2", "m1", "m2", "m3", "m4", "m5", "q2", "gq", "of"]
              + ["b%d" % i for i in range(8)] + ["pk%d" % i for i in range(7)] + ["own"]
              + ["r1", "r2", "r3", "r5", "r6", "yv0", "yv1", "ys0", "ys1"])


def bits(m):
    return [i for i in range(m.bit_length()) if m >> i & 1]


def join(b):
    return sum(1 << i for i in b)


def routes(cores, topo):
    chips = []
    for c in cores:
        if topo.chip(c) not in chips:
            chips.append(topo.chip(c))
    allchips = sorted({topo.chip(c) for c in range(SIM)})
    mate = {a: b for a in allchips for b in allchips if topo.mates(a, b)}
    on = {x: [i for i, c in enumerate(cores) if topo.chip(c) == x] for x in chips}
    used = set(cores)

    def relays(chip, die, ranks):
        found = [c for c in range(SIM) if topo.chip(c) == chip and topo.die(c) == die and c not in used
                 and all(topo.may_write(c, cores[d]) for d in ranks)]
        found = [found[min(i, len(found) - 1)] for i in range(len(ranks))]
        used.update(found)
        return found

    plan = []
    for src in cores:
        cs, die = topo.chip(src), topo.die(src)
        others = sorted((x for x in chips if x != cs), key=lambda x: (chips.index(x) - chips.index(cs)) % len(chips))
        far = [x for x in others if not topo.same_plane(cs, x) and not topo.mates(cs, x)]
        barred = [x for x in others if not topo.may_write(src, cores[on[x][0]])]
        if mate[cs] in chips and far:
            m = on[mate[cs]]
            (a0, a1), (b0, b1) = [on[x] for x in far]
            away = [(d, relays(mate[topo.chip(cores[d])], die, [d])[0]) for d in (a0, b0, a1)]
            h0, h1 = relays(cs, die, m)
            if barred:
                here = [(b1, h1), (m[0], h0), (m[1], h0)]
            else:
                here = [(m[0], h0), (m[1], h1), (b1, h1)]
        else:
            hand = (barred or [x for x in others if topo.same_plane(cs, x)])[-1]
            here = list(zip(on[hand], relays(cs, die, on[hand])))
            rest = [d for x in others if x != hand for d in on[x]]
            more = [d for d in rest if topo.same_plane(cs, topo.chip(cores[d]))][-1]
            here.append((more, relays(cs, die, [more])[0]))
            away = [(d, None) for d in rest if d != more]
        plan.append([[away[0]], [here[0]], [away[1], here[1]], [here[2]], [away[2]]])
    return plan


def jobs_of(plan, core):
    for r, calls in enumerate(plan):
        mine = [d for call in calls for d, h in call if h == core]
        if mine:
            return r, mine
    return None, []


def pieces(ds, i):
    return HALVES if i == len(ds) - 1 else WHOLE


def cuts(calls, call):
    return HALVES if call is calls[-1] and all(h is None for d, h in call) else WHOLE


def layout(plan, d):
    halved = []
    for r, calls in enumerate(plan):
        for call in calls:
            for b, h in call:
                ds = jobs_of(plan, h)[1]
                if b == d and (cuts(calls, call) if h is None else pieces(ds, ds.index(d))) is HALVES:
                    halved.append(r)
    w0 = CAPP * len(halved)
    z0 = w0 + BLK * (N - len(halved))
    at, w = {}, w0
    for r in range(N):
        if r in halved:
            i = halved.index(r)
            at[r] = (CAPP * i, z0 + CAP + CAPP * i)
        else:
            at[r] = (w, w + CAPP)
            w += BLK
    return at, w0, z0


def masks(core, topo):
    away = [c for c in range(SIM) if topo.chip(c) != topo.chip(core) and topo.may_write(core, c)][0]
    near = [c for c in range(SIM) if topo.chip(c) == topo.chip(core) and c != core][0]
    off = bits(topo.mask(core, away))
    return off, [i for i in bits(topo.mask(core, near)) if i not in off]


def engines(core, to, topo):
    off, near = masks(core, topo)
    res = []
    for i, c in enumerate(to):
        here = topo.chip(c) == topo.chip(core)
        same = [j for j, b in enumerate(to) if (topo.chip(b) == topo.chip(core)) == here]
        e = near if here else off
        w = len(e) // len(same)
        res.append(e[same.index(i) * w:(same.index(i) + 1) * w])
    return res


def ident(topo, c):
    rid, pid, _ = topo.addr(c)
    return DstId(rid=rid, pnc=pid)


def cast(T, topo, r, dsts, eng):
    at = T.xa[:, 8 * r:8 * r + 8]
    return RemoteDMATransfer(dst_ids=[ident(topo, d) for d in dsts], dma_engine_mask=join(eng), remote_sem=T.sem.meta,
                             srcs=[at], dsts=[at for d in dsts])


def relay_program(g, core, T, topo, plan, r, ds):
    off = masks(core, topo)[0]
    src = T.cores[r]
    g.wait_ge(T.sem.meta, len(engines(src, [core], topo)[0]))
    g.remote_dma_fused([cast(T, topo, r, [T.cores[d] for d in ds], off)], local_sem=T.sem.loc)
    loc = len(off)
    for i, d in enumerate(ds):
        call = [c for c in plan[r] if (d, core) in c][0]
        eng = engines(src, [T.cores[b] if h is None else h for b, h in call], topo)[call.index((d, core))]
        g.wait_ge(T.sem["rb%d" % i], len(eng))
        rid, pid, _ = topo.addr(T.cores[d])
        for a, b, s in pieces(ds, i):
            lo = layout(plan, d)[0][r][s]
            g.remote_dma(T.land[:, lo:lo + b - a], T.rb[:, i * BLK + a:i * BLK + b], T.sem["data%d" % s],
                         T.sem.loc, pid, rid, join(off))
            loc += len(off)
    g.wait_ge(T.sem.loc, loc)


def rank_program(g, core, T, topo):
    cores = list(T.cores)
    plan = routes(cores, topo)
    rank = T.rank_of(core)
    if rank is None:
        r, ds = jobs_of(plan, core)
        if ds:
            relay_program(g, core, T, topo, plan, r, ds)
        return
    S = T.sem
    V, A, P, Y = g.vector, g.scalar, g.tensor, g.sync
    op = AluOpType
    mine = plan[rank]
    partner = [i for i, c in enumerate(cores) if topo.chip(c) == topo.chip(core) and i != rank][0]
    off, near = masks(core, topo)
    meta_total = len(near)
    data_total = [len(near), 0]
    for r in range(N):
        for call in plan[r]:
            to = [cores[d] if h is None else h for d, h in call]
            for (d, h), e in zip(call, engines(cores[r], to, topo)):
                if d == rank:
                    full = masks(cores[r] if h is None else h, topo)[0]
                    meta_total += len(full)
                    ds = jobs_of(plan, h)[1]
                    for a, b, s in cuts(plan[r], call) if h is None else pieces(ds, ds.index(d)):
                        data_total[s] += len(e) if h is None else len(full)
    at, w0, z0 = layout(plan, rank)
    first = [0, w0]
    end = [z0 + CAP, LW]
    place = [[at[r][e] - first[e] for r in range(N)] + [z0 - first[e]] for e in range(EL)]

    ext = T.xa[:, 8 * rank:8 * rank + 8]
    Y.dma_start(ext, T.ex[:, :]).then_inc(S.exs, 16)
    Y.dma_start(T.xs[:, :], T.x[:, :]).then_inc(S.xl, 16)

    imp = {"allow_small_or_imprecise_dtypes": True}
    g.iota(T.pcol[:, :], [[0, 1]], 0, 1).then_inc(S.gi0, 1)
    g.iota(T.kf[:, :], [[0, 8], [1, 16]], 0, 0, **imp).then_inc(S.gi1, 1)
    g.iota(T.ti[:, :], [[1, 8]], 0, 0).then_inc(S.gi2, 1)
    g.iota(T.chf[:, :], [[0, 16], [1, 8]], 0, 0, **imp).then_inc(S.gi3, 1)
    g.iota(T.cf[:, :], [[1, 128]], 0, 0, **imp).then_inc(S.gi4, 1)
    targets = [cores[d] if h is None else h for call in mine for d, h in call]
    out_ = sorted({t for t in targets if topo.chip(t) != topo.chip(core)})
    in_ = sorted({t for t in targets if topo.chip(t) == topo.chip(core)}) + [cores[partner]]
    g.wait_ge(S.exs, 16)
    g.remote_dma_fused([cast(T, topo, rank, out_, off), cast(T, topo, rank, in_, near)], local_sem=S.loc)
    loc = len(off) + len(near)
    g.iota(T.c16[:, :], [[place[1][0] - place[0][0], EL], [16, CAP // 16]], place[0][0], 0, **imp).then_inc(S.gi5, 1)
    n = 0
    for call in mine:
        to = [cores[d] if h is None else h for d, h in call]
        for a, b, s in cuts(mine, call):
            tr = []
            for (d, h), c, eng in zip(call, to, engines(core, to, topo)):
                if a == 0:
                    g.wait_ge(S["pk%d" % n], 2 if n < 2 else 1)
                    n += 1
                if h is None:
                    lo = layout(plan, d)[0][rank][s]
                    sem, dst = S["data%d" % s], T.land[:, lo:lo + b - a]
                else:
                    k = jobs_of(plan, h)[1].index(d)
                    sem, dst = S["rb%d" % k], T.rb[:, k * BLK:(k + 1) * BLK]
                tr.append(RemoteDMATransfer(dst_ids=[ident(topo, c)], dma_engine_mask=join(eng), remote_sem=sem,
                                            srcs=[T.sb[:, d * BLK + a:d * BLK + b]], dsts=[dst]))
                loc += len(eng)
            g.remote_dma_fused(tr, local_sem=S.loc)
    g.wait_ge(S.pk6, 1)
    rid, pid, _ = topo.addr(cores[partner])
    lo = layout(plan, partner)[0][rank][0]
    g.remote_dma(T.land[:, lo:lo + BLK], T.sb[:, partner * BLK:(partner + 1) * BLK], S.data0, S.loc, pid, rid, join(near))
    loc += len(near)

    fn = ActivationFunctionType
    cp = fn.Copy

    def spread(eng, i):
        out, col = T.rsp[:, 128 * i:128 * (i + 1)], T.mk[:, i:i + 1]
        if eng == "v":
            V.tensor_scalar(out, T.s1[:, :], col, None, op.mult).then_inc(S.kr, 1)
        else:
            A.activation(out, T.s1[:, :], cp, scale=col).then_inc(S.kr, 1)

    A.wait_ge(S.gi1, 1)
    A.activation(T.ones[:, :], T.kf[:, :], cp, bias=1.0, scale=0.0).then_inc(S.k0, 1)
    A.activation(T.rst[:, :], T.kf[:, :], fn.Sign).then_inc(S.kc, 1)
    A.wait_ge(S.k4, 1)
    A.wait_ge(S.k9, 1)
    for i in (0, 1, 2):
        spread("s", i)
    A.wait_ge(S.gi4, 1)
    A.wait_ge(S.p2, 2)
    A.activation(T.i4a[:, :], T.cf[:, :], fn.Abs, bias=T.pf[:, 4:5], scale=-1.0).then_inc(S.k5, 1)
    A.wait_ge(S.k5, 1)
    A.activation(T.i4[:, :], T.i4a[:, :], fn.Relu, bias=BIG, scale=-BIG).then_inc(S.kd, 1)

    V.wait_ge(S.gi0, 1)
    for i, (o, c) in enumerate([(op.bitwise_and, 7), (op.logical_shift_right, 3), (op.bitwise_and, 15),
                                (op.logical_shift_right, 4)]):
        V.tensor_scalar(T.pi[:, i:i + 1], T.pcol[:, :], c, None, o).then_inc(S.p1, 1)
    V.tensor_copy(T.pf[:, 4:5], T.pcol[:, :]).then_inc(S.p2, 1)
    V.wait_ge(S.p1, 4)
    V.tensor_copy(T.pf[:, 0:4], T.pi[:, :]).then_inc(S.p2, 1)
    V.wait_ge(S.gi1, 1)
    V.wait_ge(S.p2, 2)
    V.tensor_scalar(T.sc[:, 1:2], T.pf[:, 0:1], 128.0, T.pf[:, 1:2], op.mult, op.add).then_inc(S.p5, 1)
    V.tensor_scalar(T.s1[:, :], T.kf[:, :], T.pf[:, 2:3], None, op.is_equal).then_inc(S.k4, 1)
    V.wait_ge(S.gi2, 1)
    V.tensor_scalar(T.mk[:, :], T.ti[:, :], T.pf[:, 3:4], None, op.is_equal).then_inc(S.k9, 1)
    V.tensor_copy(T.tu[:, :], T.ti[:, :]).then_inc(S.k1, 1)
    V.wait_ge(S.p5, 1)
    V.tensor_scalar(T.jc[:, :], T.ti[:, :], 16.0, T.sc[:, 1:2], op.mult, op.add).then_inc(S.k2, 1)
    V.wait_ge(S.gi3, 1)
    V.tensor_scalar(T.ma[:, :], T.chf[:, :], T.pf[:, 0:1], None, op.is_gt).then_inc(S.k1, 1)
    V.tensor_scalar(T.mb[:, :], T.chf[:, :], T.pf[:, 0:1], None, op.is_equal).then_inc(S.k1, 1)
    V.wait_ge(S.k1, 3)
    V.wait_ge(S.exs, 16)
    V.tensor_tensor(T.oh[:, :], ext.indirect(T.tu[:, 0:8]), T.kf[:, :], op.is_equal).then_inc(S.o1, 1)
    V.wait_ge(S.gi4, 1)
    V.tensor_scalar(T.gt[:, :], T.cf[:, :], T.pf[:, 4:5], None, op.is_gt).then_inc(S.k8, 1)
    V.wait_ge(S.k4, 1)
    V.wait_ge(S.k8, 1)
    V.tensor_tensor(T.s2[:, :], T.s1[:, :], T.gt[:, :], op.mult).then_inc(S.k7, 1)
    V.tensor_tensor(T.mx[:, :], T.mb[:, :], T.gt[:, :], op.mult).then_inc(S.k6, 1)
    V.tensor_scalar(T.cfb[:, :], T.cf[:, :], BIG, None, op.add).then_inc(S.k2, 1)
    V.wait_ge(S.k9, 1)
    for i in (3, 4):
        spread("v", i)
    V.wait_ge(S.k2, 2)
    V.wait_ge(S.kc, 1)
    V.wait_ge(S.m1, 1)
    V.tensor_tensor_scan(T.vs[:, :], T.rst[:, :], T.pcum[:, 0:128], 0.0, op.mult, op.max).then_inc(S.q2, 1)
    V.wait_ge(S.q2, 1)
    for t in range(TV):
        V.tensor_scalar(T.lh[:, 128 * t:128 * (t + 1)], T.cfb[:, :], T.vs[:, 16 * t + 15:16 * t + 16], T.jc[:, t:t + 1],
                        op.is_equal, op.mult).then_inc(S["b%d" % t], 1)
        if t == 0:
            V.wait_ge(S.o1, 1)
            for u in range(TV, 8):
                V.tensor_scalar(T.ohj[:, 16 * u:16 * (u + 1)], T.oh[:, 16 * u:16 * (u + 1)], T.jc[:, u:u + 1], None,
                                op.mult).then_inc(S.oj, 1)
    V.wait_ge(S.m2, 1)
    V.tensor_copy(T.gf[:, :], T.pg[:, 0:16]).then_inc(S.gq, 1)
    V.wait_ge(S.m5, 1)
    V.tensor_copy(T.offs[:, :], T.pidx[:, 0:128]).then_inc(S.of, 1)

    A.wait_ge(S.h1, 1)
    A.activation(T.x1[:, :], T.px1[:, 0:128], cp).then_inc(S.w1, 1)
    A.wait_ge(S.h2, 1)
    A.activation(T.x2[:, :], T.px2[:, 0:128], cp).then_inc(S.w2, 1)
    A.activation(T.cfs[:, :], T.cf[:, :], cp, bias=BIG).then_inc(S.ks, 1)
    spread("s", 5)
    A.wait_ge(S.ks, 1)
    A.wait_ge(S.q2, 1)
    for t in range(TV, 8):
        A.activation(T.za[:, 128 * t:128 * (t + 1)], T.cfs[:, :], fn.Abs, bias=T.vs[:, 16 * t + 15:16 * t + 16],
                     scale=-1.0).then_inc(S.z6, 1)
    A.wait_ge(S.z6, 8 - TV)
    for t in range(TV, 8):
        A.activation(T.ls[:, 128 * t:128 * (t + 1)], T.za[:, 128 * t:128 * (t + 1)], fn.Relu, bias=1.0,
                     scale=-1.0).then_inc(S["b%d" % t], 1)
    for i in (6, 7):
        spread("s", i)

    P.wait_ge(S.k1, 3)
    P.wait_ge(S.o1, 1)
    P.matmul(T.px1[:, 0:128], T.oh[:, :], T.ma[:, :], True, True).then_inc(S.h1, 1)
    P.matmul(T.px2[:, 0:128], T.oh[:, :], T.mb[:, :], True, True).then_inc(S.h2, 1)
    P.wait_ge(S.kd, 1)
    P.matmul(T.pcum[:, 0:128], T.i4[:, :], T.oh[:, :], True, False)
    P.wait_ge(S.k4, 1)
    P.wait_ge(S.w1, 1)
    P.matmul(T.pcum[:, 0:128], T.x1[:, :], T.s1[:, :], False, False)
    P.wait_ge(S.k7, 1)
    P.wait_ge(S.w2, 1)
    P.matmul(T.pcum[:, 0:128], T.x2[:, :], T.s2[:, :], False, False)
    P.wait_ge(S.k6, 1)
    P.matmul(T.pcum[:, 0:128], T.mx[:, :], T.oh[:, :], False, True).then_inc(S.m1, 1)
    turn = list(range(4)) + list(range(TV, 8)) + list(range(4, TV))
    for t in turn:
        P.wait_ge(S["b%d" % t], 1)
        if t == TV:
            P.wait_ge(S.oj, 8 - TV)
        lhs, rhs = (T.lh, T.oh) if t < TV else (T.ls, T.ohj)
        m = P.matmul(T.pg[:, 0:16], lhs[:, 128 * t:128 * (t + 1)], rhs[:, 16 * t:16 * (t + 1)], t == turn[0], t == turn[-1])
    m.then_inc(S.m2, 1)
    P.wait_ge(S.kr, 8)
    P.wait_ge(S.gq, 1)
    for i in range(8):
        m = P.matmul(T.pidx[:, i:128:8], T.rsp[:, 128 * i:128 * (i + 1)], T.gf[:, :], True, True)
    m.then_inc(S.m5, 1)

    def pack(eng, d, out, sem, a=0, b=BLK):
        src = T.xs[:, 0:1024].indirect(T.offs[:, (BLK * d + a) // 16:(BLK * d + b) // 16])
        if eng == "v":
            V.tensor_copy(out[:, a:b], src).then_inc(sem, 1)
        else:
            A.activation(out[:, a:b], src, cp, bias=-0.0).then_inc(sem, 1)

    for q in (V, A):
        q.wait_ge(S.of, 1)
        q.wait_ge(S.xl, 16)
    order = [d for call in mine for d, h in call] + [partner]
    for i, d in enumerate(order):
        out = T.sb[:, d * BLK:(d + 1) * BLK]
        if i < 2:
            pack("v", d, out, S["pk%d" % i], 0, CAPP)
            pack("s", d, out, S["pk%d" % i], CAPP, BLK)
        else:
            pack("vs"[i % 2], d, out, S["pk%d" % i])
    pack("s", rank, T.land[:, at[rank][0]:at[rank][0] + BLK], S.own)

    nq = 0
    for e in range(EL):
        step = [place[e][r + 1] - place[e][r] for r in range(N)]
        r = 0
        while r < N:
            q = r
            while q < N and step[q] == step[r]:
                q += 1
            A.activation(T.dr[0:1, 128 * e + 16 * r:128 * e + 16 * q], T.kf[0:1, 16 * r:16 * q], cp, bias=float(step[r]),
                         scale=0.0).then_inc(S.kq, 1)
            nq += 1
            r = q
    V.memset(T.land[:, z0:z0 + CAP], 0.0).then_inc(S.kz, 1)
    V.tensor_scalar(T.sc[:, 2:3], T.pf[:, 1:2], 16.0, None, op.mult).then_inc(S.p6, 1)
    V.tensor_scalar(T.sc[:, 3:4], T.pf[:, 1:2], 16.0, 16.0, op.mult, op.add).then_inc(S.p6, 1)
    V.wait_ge(S.p6, 2)
    V.wait_ge(S.gi5, 1)
    V.tensor_scalar(T.le[:, :], T.cf[:, :], T.sc[:, 2:3], None, op.is_ge).then_inc(S.k3, 1)
    V.tensor_scalar(T.nle[:, :], T.cf[:, :], T.sc[:, 2:3], -1.0, op.is_ge, op.mult).then_inc(S.k3, 1)
    V.tensor_scalar(T.lt[:, :], T.cf[:, :], T.sc[:, 3:4], None, op.is_ge).then_inc(S.k3, 1)
    V.tensor_scalar(T.rr[:, :], T.kf[:, :], T.pf[:, 2:3], None, op.is_equal).then_inc(S.k3, 1)
    V.tensor_scalar(T.bas[:, :], T.c16[:, :], T.pf[:, 2:3], None, op.add).then_inc(S.k3, 1)
    V.tensor_scalar(T.ip[:, :], T.c16[:, 0:30], T.pf[:, 2:3], float(place[0][0]), op.add,
                    op.subtract).then_inc(S.k3, 1)
    V.wait_ge(S.meta, meta_total)
    for e in range(EL):
        V.tensor_scalar(T.eqx[:, 64 * e:64 * (e + 1)], T.xa[:, :], float(EL * rank + e), None,
                        op.is_equal).then_inc(S.r1, 1)
    P.wait_ge(S.k3, 6)
    P.matmul(T.prix[:, 0:60], T.rr[0:16, :], T.bas[0:16, :], True, False)
    P.wait_ge(S.k0, 1)
    P.wait_ge(S.r1, 2)
    for e in range(EL):
        m = P.matmul(T.pcnt[0:64, 4 + e:5 + e], T.eqx[:, 64 * e:64 * (e + 1)], T.ones[:, 0:1], True, True)
    m.then_inc(S.r2, 1)
    V.wait_ge(S.r2, 1)
    V.tensor_copy(T.cnb[0:64, :], T.pcnt[0:64, 4:6]).then_inc(S.r3, 1)
    P.wait_ge(S.r3, 1)
    P.matmul(T.pcnt[:, 0:2], T.le[0:64, :], T.cnb[0:64, :], True, True)
    P.wait_ge(S.kq, nq)
    for e in range(EL):
        P.matmul(T.pcnt[:, 2 + e:3 + e], T.dr[0:1, 128 * e:128 * (e + 1)], T.ones[0:1, 0:1], True, False)
        P.matmul(T.pcnt[:, 2 + e:3 + e], T.nle[0:64, :], T.cnb[0:64, e:e + 1], False, False)
        m = P.matmul(T.pcnt[:, 2 + e:3 + e], T.lt[0:64, :], T.cnb[0:64, e:e + 1], False, True)
    m.then_inc(S.m3, 1)
    V.wait_ge(S.k3, 6)
    V.wait_ge(S.m3, 1)
    for e in range(EL):
        V.tensor_scalar(T.st[:, 30 * e:30 * (e + 1)], T.ip[:, :], T.pcnt[:, e:e + 1], T.pcnt[:, 2 + e:3 + e], op.is_ge,
                        op.mult).then_inc(S.r5, 1)
    P.wait_ge(S.r5, 2)
    P.matmul(T.prix[:, 0:60], T.rr[:, :], T.st[:, :], False, True).then_inc(S.m4, 1)
    V.wait_ge(S.m4, 1)
    V.tensor_copy(T.ro[:, :], T.prix[:, 0:60]).then_inc(S.r6, 1)

    for q in (V, A):
        q.wait_ge(S.r6, 1)
        q.wait_ge(S.kz, 1)
        q.wait_ge(S.own, 1)
    hc = HALF // 16
    for e, y in enumerate((T.y0, T.y1)):
        if data_total[e]:
            V.wait_ge(S["data%d" % e], data_total[e])
            A.wait_ge(S["data%d" % e], data_total[e])
        win = T.land[:, first[e]:end[e]]
        V.tensor_copy(y[:, 0:HALF], win.indirect(T.ro[:, 30 * e:30 * e + hc])).then_inc(S["yv%d" % e], 1)
        A.activation(y[:, HALF:CAP], win.indirect(T.ro[:, 30 * e + hc:30 * (e + 1)]), cp,
                     bias=-0.0).then_inc(S["ys%d" % e], 1)
    for e, y in enumerate((T.y0, T.y1)):
        Y.wait_ge(S["yv%d" % e], 1)
        Y.wait_ge(S["ys%d" % e], 1)
        Y.dma_start(T.y[:, CAP * e:CAP * (e + 1)], y[:, :]).then_inc(S.sta, 16)
    Y.wait_ge(S.sta, 32)
    g.wait_ge(S.loc, loc)
